import numpy as np
import ml_dtypes


def mxq(x, axis, fmt="e4m3"):
    dtype, down = {"e4m3": (ml_dtypes.float8_e4m3fn, 7), "e5m2": (ml_dtypes.float8_e5m2, 14)}[fmt]
    v = np.moveaxis(np.asarray(x, np.float32).astype(ml_dtypes.bfloat16).astype(np.float64), axis, -1)
    blocks = v.reshape(v.shape[:-1] + (-1, 32))
    amax = np.abs(blocks).max(-1, keepdims=True)
    byte = np.maximum(np.where(amax > 0, np.frexp(amax)[1] - 1 + 127, 0) - down, 1)
    scale = np.exp2(byte - 127.0)
    codes = (blocks / scale).astype(np.float32).astype(dtype).astype(np.float64)
    return np.moveaxis((codes * scale).reshape(v.shape), -1, axis)


WIDE = False


def mx_kscale(k):
    if not WIDE:
        return np.ones(k)
    levels = np.array([10, -10, 5, -5, 0])
    if k % 512:
        return np.exp2(np.random.permutation(np.resize(levels, k // 32))).repeat(32)
    a = np.empty((k // 512, 16))
    for p in range(k // 512):
        a[p, :8] = np.random.permutation(np.resize(levels, 8))
        for g in range(8):
            far = levels[np.abs(levels - a[p, g]) >= 10]
            a[p, g + 8] = far[np.random.randint(len(far))]
    return np.exp2(a.ravel()).repeat(32)


def f64(x):
    return np.asarray(x).astype(np.float64)


def striped(idx):
    return np.tile(idx.reshape(-1, 16).T, (8, 1)).astype(np.uint16)


def unstriped(offs):
    return offs[:16].T.reshape(-1).astype(np.int64)


def pack_weight(w):
    k, n = w.shape
    w = f64(np.asarray(w, np.float32).astype(ml_dtypes.bfloat16)).reshape(k // 32, 32, n)
    amax = np.abs(w).max(1)
    byte = np.clip(np.where(amax > 0, np.frexp(amax)[1] - 1 + 127 - 7, 1), 1, 254)
    scaled = (w * np.exp2(127.0 - byte)[:, None, :]).reshape(k, n).astype(np.float32)
    words = np.ascontiguousarray(scaled.reshape(k // 512, 128, 4, n).transpose(0, 1, 3, 2)).astype(ml_dtypes.float8_e4m3fn).view(np.uint8)
    return words, np.ascontiguousarray(byte.astype(np.uint8).reshape(k // 512, 16, n))


def unpack_weight(words, scales):
    g, p, n, _ = words.shape
    vals = np.ascontiguousarray(words).view(ml_dtypes.float8_e4m3fn).astype(np.float64) * np.repeat(np.exp2(scales.astype(np.float64) - 127.0), 8, axis=1)[..., None]
    return vals.transpose(0, 1, 3, 2).reshape(g * 512, n)


E2M1 = np.array([0.0, 0.5, 1.0, 1.5, 2.0, 3.0, 4.0, 6.0, -0.0, -0.5, -1.0, -1.5, -2.0, -3.0, -4.0, -6.0])


def pack_fp4(w):
    k, n = w.shape
    w = f64(np.asarray(w, np.float32).astype(ml_dtypes.bfloat16)).reshape(k // 32, 32, n)
    amax = np.abs(w).max(1)
    mant, ex = np.frexp(amax / 6.0)
    byte = np.clip(np.where(amax > 0, np.where(mant > 0.5, ex, ex - 1) + 127, 1), 1, 254)
    scaled = (w * np.exp2(127.0 - byte)[:, None, :]).reshape(k, n).astype(np.float32)
    c = np.ascontiguousarray(scaled.reshape(k // 512, 128, 4, n).transpose(0, 1, 3, 2)).astype(ml_dtypes.float4_e2m1fn).view(np.uint8) & 0xF
    words = (c[..., 0::2] | (c[..., 1::2] << 4)).reshape(k // 512, 128, 2 * n)
    return np.ascontiguousarray(words), np.ascontiguousarray(byte.astype(np.uint8).reshape(k // 512, 16, n))


def unpack_fp4(words, scales):
    g, _, n = scales.shape
    words = np.ascontiguousarray(words).reshape(g, 128, n, 2)
    nib = np.empty((g, 128, n, 4), np.uint8)
    nib[..., 0::2] = words & 0xF
    nib[..., 1::2] = words >> 4
    vals = E2M1[nib] * np.repeat(np.exp2(scales.astype(np.float64) - 127.0), 8, axis=1)[..., None]
    return vals.transpose(0, 1, 3, 2).reshape(g * 512, n)


K, T, S, H, N = 512, 1024, 512, 512, 256


def setup_inputs():
    n = np.random.standard_normal
    s = mx_kscale(K)[:, None]
    u = mx_kscale(H)
    packed_xT = pack_weight(n((K, T)) * s)
    packed_w2 = pack_fp4(n((H, N)) / np.sqrt(H) / u[:, None])
    return {
        "x_words": packed_xT[0],
        "x_scales": packed_xT[1],
        "w1": (n((K, H)) / np.sqrt(K) / s * u).astype(np.float32),
        "w2_words": packed_w2[0],
        "w2_scales": packed_w2[1],
        "offs": striped(np.random.permutation(T)[:S]),
    }


def reference(x_words, x_scales, w1, w2_words, w2_scales, offs):
    xq = unpack_weight(x_words, x_scales)[:, unstriped(offs)]
    h = mxq(f64(w1), 0, "e4m3").T @ xq
    z = h - h.mean(axis=1, keepdims=True)
    return unpack_fp4(w2_words, w2_scales).T @ mxq(z, 0, "e4m3")

@@ -1,0 +1,191 @@
+from contextlib import ExitStack
+
+import concourse.mybir as mybir
+
+K, T, S, H, N = 512, 1024, 512, 512, 256
+FLOPS = 2 * K * H * S + 2 * H * N * S
+
+F32 = mybir.dt.float32
+BF16 = mybir.dt.bfloat16
+I32 = mybir.dt.int32
+U32 = mybir.dt.uint32
+U16 = mybir.dt.uint16
+U8 = mybir.dt.uint8
+FP8X4 = mybir.dt.float8_e4m3fn_x4
+FP4X4 = mybir.dt.float4_e2m1fn_x4
+MULT = mybir.AluOpType.mult
+ADD = mybir.AluOpType.add
+COPY = mybir.ActivationFunctionType.Copy
+IDENT = mybir.ActivationFunctionType.Identity
+
+P = 128
+PACK = 4
+HALF = S // 2
+PIECE = 128
+
+
+def load_scale_rows(queue, plane, rows):
+    for q in range(4):
+        queue.dma_start(out=plane[32 * q : 32 * q + 4, :].bitcast(I32), in_=rows[4 * q : 4 * q + 4, :].bitcast(I32))
+
+
+def tile_picked_deepset_none_p_kernel(tc, x_words, x_scales, w1, w2_words, w2_scales, offs, out):
+    nc = tc.nc
+    with ExitStack() as ctx:
+        sb = ctx.enter_context(tc.tile_pool(name="sb", bufs=1))
+        ps = ctx.enter_context(tc.psum_pool(name="ps", bufs=1))
+
+        offsets = sb.tile([P, S // 16], U16, name="offsets")
+        x_table = sb.tile([P, T], I32, name="x_table", align_bytes=64)
+        xs_table = sb.tile([P, T], U8, name="xs_table", align_bytes=64)
+        w1_raw = sb.tile([P, PACK, H], F32, name="w1_raw", align_bytes=64)
+        w2_codes = sb.tile([P, 2 * N], U8, name="w2_codes", align_bytes=64)
+        w2_plane = sb.tile([P, N], U8, name="w2_plane", align_bytes=64)
+
+        nc.vector.memset(xs_table[:].bitcast(I32), 0)
+        nc.vector.memset(w2_plane[:].bitcast(I32), 0)
+        w1_rows = w1.rearrange("(p j) c -> p j c", j=PACK)
+        nc.sync.dma_start(out=w1_raw[:, 0:2, :], in_=w1_rows[:, 0:2, :])
+        nc.sync.dma_start(offsets[:], offs)
+        load_scale_rows(nc.sync, xs_table, x_scales[0])
+        nc.sync.dma_start(out=w1_raw[:, 2:4, :], in_=w1_rows[:, 2:4, :])
+        nc.sync.dma_start(out=x_table[:], in_=x_words[0].rearrange("p n r -> p (n r)").bitcast(I32))
+        nc.sync.dma_start(out=w2_codes[:].bitcast(I32), in_=w2_words[0].bitcast(I32))
+        load_scale_rows(nc.sync, w2_plane, w2_scales[0])
+
+        xs_picked = sb.tile([P, S], U8, name="xs_picked", align_bytes=64)
+        nc.vector.tensor_copy(xs_picked[:], xs_table[:].indirect(offsets[:]))
+
+        w1_src = w1_raw[:].rearrange("p j (m t) -> p m t j", t=PACK)
+        w1_bf = [sb.tile([P, 2, P, PACK], BF16, name=f"w1_bf{u}", align_bytes=64) for u in range(2)]
+        w1_codes = [sb.tile([P, P], U32, name=f"w1_codes{t}", align_bytes=64) for t in range(PACK)]
+        w1_plane = [sb.tile([P, P], U8, name=f"w1_plane{t}", align_bytes=64) for t in range(PACK)]
+        nc.vector.tensor_copy(out=w1_bf[0][:].rearrange("p t m j -> p m t j"), in_=w1_src[:, :, 0:2, :])
+        nc.scalar.activation(out=w1_bf[1][:].rearrange("p t m j -> p m t j"), in_=w1_src[:, :, 2:4, :], func=COPY)
+
+        def quantize_w1(t):
+            nc.vector.quantize_mx(
+                out=w1_codes[t][:].bitcast(FP8X4),
+                scales=w1_plane[t][:],
+                in_=w1_bf[t // 2][:, t % 2, :, :].rearrange("p m j -> p (m j)"),
+            )
+
+        x_picked = sb.tile([P, S], U32, name="x_picked", align_bytes=64)
+
+        def gather_words(a):
+            cols = HALF // 16
+            nc.vector.tensor_copy(x_picked[:, a * HALF : (a + 1) * HALF], x_table[:].bitcast(U32).indirect(offsets[:, a * cols : (a + 1) * cols]))
+
+        quantize_w1(0)
+        quantize_w1(1)
+        gather_words(0)
+        gather_words(1)
+        quantize_w1(3)
+        quantize_w1(2)
+
+        scaled = [sb.tile([P, S], F32, name=f"scaled{t}", align_bytes=64) for t in range(PACK)]
+        partial = sb.tile([P, PACK], F32, name="partial")
+        neg_mean = sb.tile([P, PACK], F32, name="neg_mean")
+        whole_tile = sb.tile([P, 1], F32, name="whole_tile")
+        whole_mean = whole_tile[:]
+        z_planes = sb.tile([P, PACK, S], BF16, name="z_planes", align_bytes=64)
+
+        def first_product(t, cols, bank_no):
+            bank = ps.tile([P, cols.stop - cols.start], F32, name=f"h{bank_no}", tag=f"bank{bank_no}")
+            nc.tensor.matmul_mx(
+                out=bank[:],
+                lhsT=w1_codes[t][:].bitcast(FP8X4),
+                lhsT_scale=w1_plane[t][:],
+                rhs=x_picked[:, cols].bitcast(FP8X4),
+                rhs_scale=xs_picked[:, cols],
+                start=True,
+                stop=True,
+            )
+            if cols.start == 0:
+                total = whole_mean if cols.stop == S else partial[:, t : t + 1]
+                nc.scalar.activation(out=scaled[t][:, cols], in_=bank[:], func=COPY, scale=-1.0 / S, accum_out=total)
+            else:
+                nc.vector.tensor_scalar(
+                    out=scaled[t][:, cols],
+                    in0=bank[:],
+                    scalar1=-1.0 / S,
+                    scalar2=partial[:, t : t + 1],
+                    op0=MULT,
+                    op1=ADD,
+                    accum_out=neg_mean[:, t : t + 1],
+                )
+
+        def centre(t):
+            if t == 2:
+                nc.scalar.activation(
+                    out=z_planes[:, t, :], in_=scaled[t][:], func=IDENT, scale=-float(S), bias=whole_mean
+                )
+            else:
+                nc.vector.tensor_scalar(
+                    out=z_planes[:, t, :],
+                    in0=scaled[t][:],
+                    scalar1=-float(S),
+                    scalar2=neg_mean[:, t : t + 1],
+                    op0=MULT,
+                    op1=ADD,
+                )
+
+        front, back, both = slice(0, HALF), slice(HALF, S), slice(0, S)
+        first_product(0, front, 0)
+        first_product(1, front, 1)
+        first_product(0, back, 2)
+        first_product(1, back, 3)
+        first_product(3, front, 4)
+        centre(0)
+        first_product(2, both, 5)
+        centre(1)
+        first_product(3, back, 6)
+        centre(2)
+        centre(3)
+
+        pieces = S // PIECE
+        z_bf = [sb.tile([P, PIECE, PACK], BF16, name=f"z_bf{c}", align_bytes=64) for c in range(pieces)]
+        z_codes = [sb.tile([P, PIECE], U32, name=f"z_codes{c}", align_bytes=64) for c in range(pieces)]
+        z_plane = [sb.tile([P, PIECE], U8, name=f"z_plane{c}", align_bytes=64) for c in range(pieces)]
+        out_view = out.rearrange("(m p) n -> p m n", p=P)
+
+        def weave(c, lo, hi, on_scalar):
+            src = z_planes[:, :, c * PIECE + lo : c * PIECE + hi].rearrange("p t n -> p n t")
+            if on_scalar:
+                nc.scalar.copy(out=z_bf[c][:, lo:hi, :], in_=src)
+            else:
+                nc.vector.tensor_copy(out=z_bf[c][:, lo:hi, :], in_=src)
+
+        def second_product(c):
+            nc.vector.quantize_mx(
+                out=z_codes[c][:].bitcast(FP8X4),
+                scales=z_plane[c][:],
+                in_=z_bf[c][:].rearrange("p n t -> p (n t)"),
+            )
+            bank = ps.tile([P, N // P, PIECE], F32, name=f"o{c}", tag=f"bank{c}")
+            for m in range(N // P):
+                nc.tensor.matmul_mx(
+                    out=bank[:, m, :],
+                    lhsT=w2_codes[:, 2 * P * m : 2 * P * (m + 1)].bitcast(FP4X4),
+                    lhsT_scale=w2_plane[:, P * m : P * (m + 1)],
+                    rhs=z_codes[c][:].bitcast(FP8X4),
+                    rhs_scale=z_plane[c][:],
+                    start=True,
+                    stop=True,
+                )
+            result = sb.tile([P, N // P, PIECE], F32, name=f"result{c}")
+            if c == pieces - 1:
+                nc.vector.tensor_copy(out=result[:], in_=bank[:])
+            else:
+                nc.scalar.copy(out=result[:], in_=bank[:])
+            nc.sync.dma_start(out=out_view[:, :, c * PIECE : (c + 1) * PIECE], in_=result[:])
+
+        weave(0, 0, PIECE, False)
+        weave(1, 0, PIECE, True)
+        second_product(0)
+        weave(2, 0, PIECE, False)
+        second_product(1)
+        weave(3, 0, PIECE // 2, True)
+        weave(3, PIECE // 2, PIECE, False)
+        second_product(2)
+        second_product(3)

@@ -36,19 +36,19 @@ def tile_picked_deepset_none_p_kernel(tc, x_words, x_scales, w1, w2_words, w2_sc
         ps = ctx.enter_context(tc.psum_pool(name="ps", bufs=1))
 
         offsets = sb.tile([P, S // 16], U16, name="offsets")
-        x_table = sb.tile([P, T], I32, name="x_table", align_bytes=64)
+        x_table = sb.tile([P, T], I32, name="x_table", tag="x_table", align_bytes=64)
         xs_table = sb.tile([P, T], U8, name="xs_table", align_bytes=64)
-        w1_raw = sb.tile([P, PACK, H], F32, name="w1_raw", align_bytes=64)
+        w1_raw = [sb.tile([P, 2, H], F32, name=f"w1_raw{u}", align_bytes=64) for u in range(2)]
         w2_codes = sb.tile([P, 2 * N], U8, name="w2_codes", align_bytes=64)
         w2_plane = sb.tile([P, N], U8, name="w2_plane", align_bytes=64)
 
         nc.vector.memset(xs_table[:].bitcast(I32), 0)
         nc.vector.memset(w2_plane[:].bitcast(I32), 0)
         w1_rows = w1.rearrange("(p j) c -> p j c", j=PACK)
-        nc.sync.dma_start(out=w1_raw[:, 0:2, :], in_=w1_rows[:, 0:2, :])
+        nc.sync.dma_start(out=w1_raw[0][:], in_=w1_rows[:, 0:2, :])
         nc.sync.dma_start(offsets[:], offs)
         load_scale_rows(nc.sync, xs_table, x_scales[0])
-        nc.sync.dma_start(out=w1_raw[:, 2:4, :], in_=w1_rows[:, 2:4, :])
+        nc.sync.dma_start(out=w1_raw[1][:], in_=w1_rows[:, 2:4, :])
         nc.sync.dma_start(out=x_table[:], in_=x_words[0].rearrange("p n r -> p (n r)").bitcast(I32))
         nc.sync.dma_start(out=w2_codes[:].bitcast(I32), in_=w2_words[0].bitcast(I32))
         load_scale_rows(nc.sync, w2_plane, w2_scales[0])
@@ -56,16 +56,19 @@ def tile_picked_deepset_none_p_kernel(tc, x_words, x_scales, w1, w2_words, w2_sc
         xs_picked = sb.tile([P, S], U8, name="xs_picked", align_bytes=64)
         nc.vector.tensor_copy(xs_picked[:], xs_table[:].indirect(offsets[:]))
 
-        w1_src = w1_raw[:].rearrange("p j (m t) -> p m t j", t=PACK)
+        w1_src = [tile[:].rearrange("p j (m t) -> p m t j", t=PACK) for tile in w1_raw]
         w1_bf = [sb.tile([P, 2, P, PACK], BF16, name=f"w1_bf{u}", align_bytes=64) for u in range(2)]
-        w1_codes = [sb.tile([P, P], U32, name=f"w1_codes{t}", align_bytes=64) for t in range(PACK)]
+        w1_codes = [sb.tile([P, P], U32, name=f"w1_codes{t}", align_bytes=64)[:] for t in range(2)]
         w1_plane = [sb.tile([P, P], U8, name=f"w1_plane{t}", align_bytes=64) for t in range(PACK)]
-        nc.vector.tensor_copy(out=w1_bf[0][:].rearrange("p t m j -> p m t j"), in_=w1_src[:, :, 0:2, :])
-        nc.scalar.activation(out=w1_bf[1][:].rearrange("p t m j -> p m t j"), in_=w1_src[:, :, 2:4, :], func=COPY)
+        w1_dst = [tile[:].rearrange("p t m j -> p m t j") for tile in w1_bf]
+        nc.scalar.activation(out=w1_dst[0][:, :, :, 0:2], in_=w1_src[0][:, :, 0:2, :], func=COPY)
+        nc.scalar.activation(out=w1_dst[1][:, :, :, 0:2], in_=w1_src[0][:, :, 2:4, :], func=COPY)
+        nc.vector.tensor_copy(out=w1_dst[0][:, :, :, 2:4], in_=w1_src[1][:, :, 0:2, :])
+        nc.scalar.activation(out=w1_dst[1][:, :, :, 2:4], in_=w1_src[1][:, :, 2:4, :], func=COPY)
 
         def quantize_w1(t):
             nc.vector.quantize_mx(
-                out=w1_codes[t][:].bitcast(FP8X4),
+                out=w1_codes[t].bitcast(FP8X4),
                 scales=w1_plane[t][:],
                 in_=w1_bf[t // 2][:, t % 2, :, :].rearrange("p m j -> p (m j)"),
             )
@@ -80,6 +83,8 @@ def tile_picked_deepset_none_p_kernel(tc, x_words, x_scales, w1, w2_words, w2_sc
         quantize_w1(1)
         gather_words(0)
         gather_words(1)
+        late_codes = sb.tile([P, 2, P], U32, name="late_codes", tag="x_table", align_bytes=64)
+        w1_codes.extend(late_codes[:, u, :] for u in range(2))
         quantize_w1(3)
         quantize_w1(2)
 
@@ -88,13 +93,13 @@ def tile_picked_deepset_none_p_kernel(tc, x_words, x_scales, w1, w2_words, w2_sc
         neg_mean = sb.tile([P, PACK], F32, name="neg_mean")
         whole_tile = sb.tile([P, 1], F32, name="whole_tile")
         whole_mean = whole_tile[:]
-        z_planes = sb.tile([P, PACK, S], BF16, name="z_planes", align_bytes=64)
+        z_planes = sb.tile([P, 2, PACK, HALF], BF16, name="z_planes", align_bytes=64)
 
         def first_product(t, cols, bank_no):
             bank = ps.tile([P, cols.stop - cols.start], F32, name=f"h{bank_no}", tag=f"bank{bank_no}")
             nc.tensor.matmul_mx(
                 out=bank[:],
-                lhsT=w1_codes[t][:].bitcast(FP8X4),
+                lhsT=w1_codes[t].bitcast(FP8X4),
                 lhsT_scale=w1_plane[t][:],
                 rhs=x_picked[:, cols].bitcast(FP8X4),
                 rhs_scale=xs_picked[:, cols],
@@ -115,20 +120,14 @@ def tile_picked_deepset_none_p_kernel(tc, x_words, x_scales, w1, w2_words, w2_sc
                     accum_out=neg_mean[:, t : t + 1],
                 )
 
-        def centre(t):
-            if t == 2:
-                nc.scalar.activation(
-                    out=z_planes[:, t, :], in_=scaled[t][:], func=IDENT, scale=-float(S), bias=whole_mean
-                )
+        def centre(t, halves):
+            dst = z_planes[:, halves, t, :]
+            src = scaled[t][:].rearrange("p (a n) -> p a n", a=2)[:, halves, :]
+            if t == 3:
+                nc.scalar.activation(out=dst, in_=src, func=IDENT, scale=-float(S), bias=neg_mean[:, t : t + 1])
             else:
-                nc.vector.tensor_scalar(
-                    out=z_planes[:, t, :],
-                    in0=scaled[t][:],
-                    scalar1=-float(S),
-                    scalar2=neg_mean[:, t : t + 1],
-                    op0=MULT,
-                    op1=ADD,
-                )
+                shift = whole_mean if t == 2 else neg_mean[:, t : t + 1]
+                nc.vector.tensor_scalar(out=dst, in0=src, scalar1=-float(S), scalar2=shift, op0=MULT, op1=ADD)
 
         front, back, both = slice(0, HALF), slice(HALF, S), slice(0, S)
         first_product(0, front, 0)
@@ -136,12 +135,13 @@ def tile_picked_deepset_none_p_kernel(tc, x_words, x_scales, w1, w2_words, w2_sc
         first_product(0, back, 2)
         first_product(1, back, 3)
         first_product(3, front, 4)
-        centre(0)
+        centre(0, slice(0, 2))
         first_product(2, both, 5)
-        centre(1)
+        centre(1, slice(0, 2))
         first_product(3, back, 6)
-        centre(2)
-        centre(3)
+        for a in range(2):
+            centre(2, slice(a, a + 1))
+            centre(3, slice(a, a + 1))
 
         pieces = S // PIECE
         z_bf = [sb.tile([P, PIECE, PACK], BF16, name=f"z_bf{c}", align_bytes=64) for c in range(pieces)]
@@ -150,7 +150,8 @@ def tile_picked_deepset_none_p_kernel(tc, x_words, x_scales, w1, w2_words, w2_sc
         out_view = out.rearrange("(m p) n -> p m n", p=P)
 
         def weave(c, lo, hi, on_scalar):
-            src = z_planes[:, :, c * PIECE + lo : c * PIECE + hi].rearrange("p t n -> p n t")
+            start = (c % 2) * PIECE
+            src = z_planes[:, c // 2, :, start + lo : start + hi].rearrange("p t n -> p n t")
             if on_scalar:
                 nc.scalar.copy(out=z_bf[c][:, lo:hi, :], in_=src)
             else:
@@ -162,10 +163,16 @@ def tile_picked_deepset_none_p_kernel(tc, x_words, x_scales, w1, w2_words, w2_sc
                 scales=z_plane[c][:],
                 in_=z_bf[c][:].rearrange("p n t -> p (n t)"),
             )
-            bank = ps.tile([P, N // P, PIECE], F32, name=f"o{c}", tag=f"bank{c}")
+            last = c == pieces - 1
+            cols = slice(c * PIECE, (c + 1) * PIECE)
+            if last:
+                banks = [ps.tile([P, PIECE], F32, name=f"o{c}{m}", tag=f"bank{c + m}")[:] for m in range(N // P)]
+            else:
+                bank = ps.tile([P, N // P, PIECE], F32, name=f"o{c}", tag=f"bank{c}")
+                banks = [bank[:, m, :] for m in range(N // P)]
             for m in range(N // P):
                 nc.tensor.matmul_mx(
-                    out=bank[:, m, :],
+                    out=banks[m],
                     lhsT=w2_codes[:, 2 * P * m : 2 * P * (m + 1)].bitcast(FP4X4),
                     lhsT_scale=w2_plane[:, P * m : P * (m + 1)],
                     rhs=z_codes[c][:].bitcast(FP8X4),
@@ -173,17 +180,22 @@ def tile_picked_deepset_none_p_kernel(tc, x_words, x_scales, w1, w2_words, w2_sc
                     start=True,
                     stop=True,
                 )
-            result = sb.tile([P, N // P, PIECE], F32, name=f"result{c}")
-            if c == pieces - 1:
-                nc.vector.tensor_copy(out=result[:], in_=bank[:])
+            if last:
+                low = sb.tile([P, PIECE], F32, name="low")
+                high = sb.tile([P, PIECE], F32, name="high")
+                nc.scalar.copy(out=low[:], in_=banks[0])
+                nc.scalar.dma_start(out=out_view[:, 0, cols], in_=low[:])
+                nc.vector.tensor_copy(out=high[:], in_=banks[1])
+                nc.sync.dma_start(out=out_view[:, 1, cols], in_=high[:])
             else:
+                result = sb.tile([P, N // P, PIECE], F32, name=f"result{c}")
                 nc.scalar.copy(out=result[:], in_=bank[:])
-            nc.sync.dma_start(out=out_view[:, :, c * PIECE : (c + 1) * PIECE], in_=result[:])
+                nc.sync.dma_start(out=out_view[:, :, cols], in_=result[:])
 
         weave(0, 0, PIECE, False)
-        weave(1, 0, PIECE, True)
+        weave(1, 0, PIECE, False)
+        weave(2, 0, PIECE, True)
         second_product(0)
-        weave(2, 0, PIECE, False)
         second_product(1)
         weave(3, 0, PIECE // 2, True)
         weave(3, PIECE // 2, PIECE, False)

@@ -38,17 +38,17 @@ def tile_picked_deepset_none_p_kernel(tc, x_words, x_scales, w1, w2_words, w2_sc
         offsets = sb.tile([P, S // 16], U16, name="offsets")
         x_table = sb.tile([P, T], I32, name="x_table", tag="x_table", align_bytes=64)
         xs_table = sb.tile([P, T], U8, name="xs_table", align_bytes=64)
-        w1_raw = [sb.tile([P, 2, H], F32, name=f"w1_raw{u}", align_bytes=64) for u in range(2)]
+        w1_raw = [sb.tile([P, PACK, H // 2], F32, name=f"w1_raw{u}", align_bytes=64) for u in range(2)]
         w2_codes = sb.tile([P, 2 * N], U8, name="w2_codes", align_bytes=64)
         w2_plane = sb.tile([P, N], U8, name="w2_plane", align_bytes=64)
 
         nc.vector.memset(xs_table[:].bitcast(I32), 0)
         nc.vector.memset(w2_plane[:].bitcast(I32), 0)
         w1_rows = w1.rearrange("(p j) c -> p j c", j=PACK)
-        nc.sync.dma_start(out=w1_raw[0][:], in_=w1_rows[:, 0:2, :])
+        nc.sync.dma_start(out=w1_raw[0][:], in_=w1_rows[:, :, : H // 2])
         nc.sync.dma_start(offsets[:], offs)
         load_scale_rows(nc.sync, xs_table, x_scales[0])
-        nc.sync.dma_start(out=w1_raw[1][:], in_=w1_rows[:, 2:4, :])
+        nc.sync.dma_start(out=w1_raw[1][:], in_=w1_rows[:, :, H // 2 :])
         nc.sync.dma_start(out=x_table[:], in_=x_words[0].rearrange("p n r -> p (n r)").bitcast(I32))
         nc.sync.dma_start(out=w2_codes[:].bitcast(I32), in_=w2_words[0].bitcast(I32))
         load_scale_rows(nc.sync, w2_plane, w2_scales[0])
@@ -56,106 +56,114 @@ def tile_picked_deepset_none_p_kernel(tc, x_words, x_scales, w1, w2_words, w2_sc
         xs_picked = sb.tile([P, S], U8, name="xs_picked", align_bytes=64)
         nc.vector.tensor_copy(xs_picked[:], xs_table[:].indirect(offsets[:]))
 
-        w1_src = [tile[:].rearrange("p j (m t) -> p m t j", t=PACK) for tile in w1_raw]
+        w1_src = [tile[:].rearrange("p j (m t) -> p m j t", t=PACK) for tile in w1_raw]
         w1_bf = [sb.tile([P, 2, P, PACK], BF16, name=f"w1_bf{u}", align_bytes=64) for u in range(2)]
-        w1_codes = [sb.tile([P, P], U32, name=f"w1_codes{t}", align_bytes=64)[:] for t in range(2)]
-        w1_plane = [sb.tile([P, P], U8, name=f"w1_plane{t}", align_bytes=64) for t in range(PACK)]
-        w1_dst = [tile[:].rearrange("p t m j -> p m t j") for tile in w1_bf]
-        nc.scalar.activation(out=w1_dst[0][:, :, :, 0:2], in_=w1_src[0][:, :, 0:2, :], func=COPY)
-        nc.scalar.activation(out=w1_dst[1][:, :, :, 0:2], in_=w1_src[0][:, :, 2:4, :], func=COPY)
-        nc.vector.tensor_copy(out=w1_dst[0][:, :, :, 2:4], in_=w1_src[1][:, :, 0:2, :])
-        nc.scalar.activation(out=w1_dst[1][:, :, :, 2:4], in_=w1_src[1][:, :, 2:4, :], func=COPY)
+        w1_codes = [sb.tile([P, 2 * P], U32, name="early_codes", align_bytes=64)]
+        w1_plane = [sb.tile([P, 2 * P], U8, name=f"w1_plane{u}", align_bytes=64) for u in range(2)]
+        w1_dst = [tile[:].rearrange("p t m j -> p m j t") for tile in w1_bf]
+        low_m, high_m = slice(0, P // 2), slice(P // 2, P)
+        nc.scalar.activation(out=w1_dst[0][:, low_m], in_=w1_src[0][:, :, :, 0:2], func=COPY)
+        nc.scalar.activation(out=w1_dst[1][:, low_m], in_=w1_src[0][:, :, :, 2:4], func=COPY)
+        nc.vector.tensor_copy(out=w1_dst[0][:, high_m], in_=w1_src[1][:, :, :, 0:2])
+        nc.scalar.activation(out=w1_dst[1][:, high_m], in_=w1_src[1][:, :, :, 2:4], func=COPY)
 
-        def quantize_w1(t):
+        def quantize_w1(u):
             nc.vector.quantize_mx(
-                out=w1_codes[t].bitcast(FP8X4),
-                scales=w1_plane[t][:],
-                in_=w1_bf[t // 2][:, t % 2, :, :].rearrange("p m j -> p (m j)"),
+                out=w1_codes[u][:].bitcast(FP8X4),
+                scales=w1_plane[u][:],
+                in_=w1_bf[u][:].rearrange("p t m j -> p (t m j)"),
             )
 
-        x_picked = sb.tile([P, S], U32, name="x_picked", align_bytes=64)
-
-        def gather_words(a):
-            cols = HALF // 16
-            nc.vector.tensor_copy(x_picked[:, a * HALF : (a + 1) * HALF], x_table[:].bitcast(U32).indirect(offsets[:, a * cols : (a + 1) * cols]))
-
         quantize_w1(0)
+
+        pieces = S // PIECE
+        x_picked = sb.tile([P, S], U32, name="x_picked", align_bytes=64)
+        for c in range(pieces):
+            nc.vector.tensor_copy(
+                x_picked[:, c * PIECE : (c + 1) * PIECE],
+                x_table[:].bitcast(U32).indirect(offsets[:, c * PIECE // 16 : (c + 1) * PIECE // 16]),
+            )
+        w1_codes.append(sb.tile([P, 2 * P], U32, name="late_codes", tag="x_table", align_bytes=64))
         quantize_w1(1)
-        gather_words(0)
-        gather_words(1)
-        late_codes = sb.tile([P, 2, P], U32, name="late_codes", tag="x_table", align_bytes=64)
-        w1_codes.extend(late_codes[:, u, :] for u in range(2))
-        quantize_w1(3)
-        quantize_w1(2)
 
         scaled = [sb.tile([P, S], F32, name=f"scaled{t}", align_bytes=64) for t in range(PACK)]
-        partial = sb.tile([P, PACK], F32, name="partial")
-        neg_mean = sb.tile([P, PACK], F32, name="neg_mean")
-        whole_tile = sb.tile([P, 1], F32, name="whole_tile")
-        whole_mean = whole_tile[:]
-        z_planes = sb.tile([P, 2, PACK, HALF], BF16, name="z_planes", align_bytes=64)
+        partial = [sb.tile([P, 1], F32, name=f"partial{t}") for t in range(2)]
+        neg_mean = [sb.tile([P, 1], F32, name=f"neg_mean{t}") for t in range(PACK)]
+        pairs = [sb.tile([P, 2, HALF, 2], BF16, name=f"pairs{a}", align_bytes=64) for a in range(2)]
+        split = (HALF, S - PIECE, S, S)
+        front_bank = [ps.tile([P, split[t]], F32, name=f"front{t}", tag=f"bank{t}") for t in range(PACK)]
+        back_bank = [ps.tile([P, S - split[t]], F32, name=f"back{t}", tag=f"bank{PACK + t}") for t in range(2)]
 
-        def first_product(t, cols, bank_no):
-            bank = ps.tile([P, cols.stop - cols.start], F32, name=f"h{bank_no}", tag=f"bank{bank_no}")
+        def first_product(t, start, width):
+            group = slice((t % 2) * P, (t % 2 + 1) * P)
+            cols = slice(start, start + width)
+            bank = front_bank[t][:, cols] if start < split[t] else back_bank[t][:, start - split[t] : start - split[t] + width]
             nc.tensor.matmul_mx(
-                out=bank[:],
-                lhsT=w1_codes[t].bitcast(FP8X4),
-                lhsT_scale=w1_plane[t][:],
+                out=bank,
+                lhsT=w1_codes[t // 2][:, group].bitcast(FP8X4),
+                lhsT_scale=w1_plane[t // 2][:, group],
                 rhs=x_picked[:, cols].bitcast(FP8X4),
                 rhs_scale=xs_picked[:, cols],
                 start=True,
                 stop=True,
             )
-            if cols.start == 0:
-                total = whole_mean if cols.stop == S else partial[:, t : t + 1]
-                nc.scalar.activation(out=scaled[t][:, cols], in_=bank[:], func=COPY, scale=-1.0 / S, accum_out=total)
+
+        def empty_front(t):
+            total = partial[t] if split[t] < S else neg_mean[t]
+            nc.scalar.activation(out=scaled[t][:, : split[t]], in_=front_bank[t][:], func=COPY, scale=-1.0 / S, accum_out=total[:])
+
+        def empty_back(t):
+            nc.vector.tensor_scalar(
+                out=scaled[t][:, split[t] :],
+                in0=back_bank[t][:],
+                scalar1=-1.0 / S,
+                scalar2=partial[t][:],
+                op0=MULT,
+                op1=ADD,
+                accum_out=neg_mean[t][:],
+            )
+
+        def centre(t, start, width, on_scalar):
+            dst = pairs[start // HALF][:, t // 2, start % HALF : start % HALF + width, t % 2]
+            src = scaled[t][:, start : start + width]
+            if not on_scalar:
+                nc.vector.tensor_scalar(out=dst, in0=src, scalar1=-float(S), scalar2=neg_mean[t][:], op0=MULT, op1=ADD)
             else:
-                nc.vector.tensor_scalar(
-                    out=scaled[t][:, cols],
-                    in0=bank[:],
-                    scalar1=-1.0 / S,
-                    scalar2=partial[:, t : t + 1],
-                    op0=MULT,
-                    op1=ADD,
-                    accum_out=neg_mean[:, t : t + 1],
-                )
+                nc.scalar.activation(out=dst, in_=src, func=IDENT, scale=-float(S), bias=neg_mean[t][:])
 
-        def centre(t, halves):
-            dst = z_planes[:, halves, t, :]
-            src = scaled[t][:].rearrange("p (a n) -> p a n", a=2)[:, halves, :]
-            if t == 3:
-                nc.scalar.activation(out=dst, in_=src, func=IDENT, scale=-float(S), bias=neg_mean[:, t : t + 1])
-            else:
-                shift = whole_mean if t == 2 else neg_mean[:, t : t + 1]
-                nc.vector.tensor_scalar(out=dst, in0=src, scalar1=-float(S), scalar2=shift, op0=MULT, op1=ADD)
+        for c in range(pieces):
+            for t in range(2):
+                first_product(t, c * PIECE, PIECE)
+        for t in range(2, PACK):
+            for a in range(2):
+                first_product(t, a * HALF, HALF)
+        for t in range(PACK):
+            empty_front(t)
+        for t in range(2):
+            empty_back(t)
+        for t in range(2):
+            centre(t, 0, HALF, False)
+            centre(t, HALF, HALF, False)
+        centre(2, 0, HALF, False)
+        centre(2, HALF, HALF, False)
+        centre(3, 0, PIECE, False)
+        centre(3, PIECE, PIECE, False)
+        centre(3, HALF, HALF, False)
 
-        front, back, both = slice(0, HALF), slice(HALF, S), slice(0, S)
-        first_product(0, front, 0)
-        first_product(1, front, 1)
-        first_product(0, back, 2)
-        first_product(1, back, 3)
-        first_product(3, front, 4)
-        centre(0, slice(0, 2))
-        first_product(2, both, 5)
-        centre(1, slice(0, 2))
-        first_product(3, back, 6)
-        for a in range(2):
-            centre(2, slice(a, a + 1))
-            centre(3, slice(a, a + 1))
-
-        pieces = S // PIECE
         z_bf = [sb.tile([P, PIECE, PACK], BF16, name=f"z_bf{c}", align_bytes=64) for c in range(pieces)]
         z_codes = [sb.tile([P, PIECE], U32, name=f"z_codes{c}", align_bytes=64) for c in range(pieces)]
         z_plane = [sb.tile([P, PIECE], U8, name=f"z_plane{c}", align_bytes=64) for c in range(pieces)]
         out_view = out.rearrange("(m p) n -> p m n", p=P)
 
-        def weave(c, lo, hi, on_scalar):
+        def weave(c, on_scalar):
             start = (c % 2) * PIECE
-            src = z_planes[:, c // 2, :, start + lo : start + hi].rearrange("p t n -> p n t")
+            words = pairs[c // 2][:].rearrange("p u n e -> p u (n e)").bitcast(F32)
+            src = words[:, :, start : start + PIECE].rearrange("p u n -> p n u")
+            dst = z_bf[c][:].rearrange("p n t -> p (n t)").bitcast(F32).rearrange("p (n u) -> p n u", u=2)
             if on_scalar:
-                nc.scalar.copy(out=z_bf[c][:, lo:hi, :], in_=src)
+                nc.scalar.copy(out=dst, in_=src)
             else:
-                nc.vector.tensor_copy(out=z_bf[c][:, lo:hi, :], in_=src)
+                nc.vector.tensor_copy(out=dst, in_=src)
 
         def second_product(c):
             nc.vector.quantize_mx(
@@ -192,12 +200,9 @@ def tile_picked_deepset_none_p_kernel(tc, x_words, x_scales, w1, w2_words, w2_sc
                 nc.scalar.copy(out=result[:], in_=bank[:])
                 nc.sync.dma_start(out=out_view[:, :, cols], in_=result[:])
 
-        weave(0, 0, PIECE, False)
-        weave(1, 0, PIECE, False)
-        weave(2, 0, PIECE, True)
-        second_product(0)
-        second_product(1)
-        weave(3, 0, PIECE // 2, True)
-        weave(3, PIECE // 2, PIECE, False)
-        second_product(2)
-        second_product(3)
+        weave(0, False)
+        weave(1, False)
+        weave(2, True)
+        weave(3, True)
+        for c in range(pieces):
+            second_product(c)

@@ -25,8 +25,8 @@ PIECE = 128
 
 
 def load_scale_rows(queue, plane, rows):
-    for q in range(4):
-        queue.dma_start(out=plane[32 * q : 32 * q + 4, :].bitcast(I32), in_=rows[4 * q : 4 * q + 4, :].bitcast(I32))
+    for r in range(4):
+        queue.dma_start(out=plane[r:P:32, :].bitcast(I32), in_=rows[r:16:4, :].bitcast(I32))
 
 
 def tile_picked_deepset_none_p_kernel(tc, x_words, x_scales, w1, w2_words, w2_scales, offs, out):
@@ -89,7 +89,7 @@ def tile_picked_deepset_none_p_kernel(tc, x_words, x_scales, w1, w2_words, w2_sc
         scaled = [sb.tile([P, S], F32, name=f"scaled{t}", align_bytes=64) for t in range(PACK)]
         partial = [sb.tile([P, 1], F32, name=f"partial{t}") for t in range(2)]
         neg_mean = [sb.tile([P, 1], F32, name=f"neg_mean{t}") for t in range(PACK)]
-        pairs = [sb.tile([P, 2, HALF, 2], BF16, name=f"pairs{a}", align_bytes=64) for a in range(2)]
+        planes = [sb.tile([P, PACK, HALF], BF16, name=f"planes{a}", align_bytes=64) for a in range(2)]
         split = (HALF, S - PIECE, S, S)
         front_bank = [ps.tile([P, split[t]], F32, name=f"front{t}", tag=f"bank{t}") for t in range(PACK)]
         back_bank = [ps.tile([P, S - split[t]], F32, name=f"back{t}", tag=f"bank{PACK + t}") for t in range(2)]
@@ -124,7 +124,7 @@ def tile_picked_deepset_none_p_kernel(tc, x_words, x_scales, w1, w2_words, w2_sc
             )
 
         def centre(t, start, width, on_scalar):
-            dst = pairs[start // HALF][:, t // 2, start % HALF : start % HALF + width, t % 2]
+            dst = planes[start // HALF][:, t, start % HALF : start % HALF + width]
             src = scaled[t][:, start : start + width]
             if not on_scalar:
                 nc.vector.tensor_scalar(out=dst, in0=src, scalar1=-float(S), scalar2=neg_mean[t][:], op0=MULT, op1=ADD)
@@ -146,8 +146,7 @@ def tile_picked_deepset_none_p_kernel(tc, x_words, x_scales, w1, w2_words, w2_sc
             centre(t, HALF, HALF, False)
         centre(2, 0, HALF, False)
         centre(2, HALF, HALF, False)
-        centre(3, 0, PIECE, False)
-        centre(3, PIECE, PIECE, False)
+        centre(3, 0, HALF, False)
         centre(3, HALF, HALF, False)
 
         z_bf = [sb.tile([P, PIECE, PACK], BF16, name=f"z_bf{c}", align_bytes=64) for c in range(pieces)]
@@ -155,11 +154,10 @@ def tile_picked_deepset_none_p_kernel(tc, x_words, x_scales, w1, w2_words, w2_sc
         z_plane = [sb.tile([P, PIECE], U8, name=f"z_plane{c}", align_bytes=64) for c in range(pieces)]
         out_view = out.rearrange("(m p) n -> p m n", p=P)
 
-        def weave(c, on_scalar):
+        def weave(c, lo, hi, on_scalar):
             start = (c % 2) * PIECE
-            words = pairs[c // 2][:].rearrange("p u n e -> p u (n e)").bitcast(F32)
-            src = words[:, :, start : start + PIECE].rearrange("p u n -> p n u")
-            dst = z_bf[c][:].rearrange("p n t -> p (n t)").bitcast(F32).rearrange("p (n u) -> p n u", u=2)
+            src = planes[c // 2][:, :, start + lo : start + hi].rearrange("p t (n i) -> p n t i", i=PACK)
+            dst = z_bf[c][:, lo:hi, :].rearrange("p (n i) t -> p n t i", i=PACK)
             if on_scalar:
                 nc.scalar.copy(out=dst, in_=src)
             else:
@@ -171,16 +169,12 @@ def tile_picked_deepset_none_p_kernel(tc, x_words, x_scales, w1, w2_words, w2_sc
                 scales=z_plane[c][:],
                 in_=z_bf[c][:].rearrange("p n t -> p (n t)"),
             )
-            last = c == pieces - 1
             cols = slice(c * PIECE, (c + 1) * PIECE)
-            if last:
-                banks = [ps.tile([P, PIECE], F32, name=f"o{c}{m}", tag=f"bank{c + m}")[:] for m in range(N // P)]
-            else:
-                bank = ps.tile([P, N // P, PIECE], F32, name=f"o{c}", tag=f"bank{c}")
-                banks = [bank[:, m, :] for m in range(N // P)]
+            result = sb.tile([P, N // P, PIECE], F32, name=f"result{c}", align_bytes=64)
             for m in range(N // P):
+                bank = ps.tile([P, PIECE], F32, name=f"o{c}{m}", tag=f"bank{2 * c + m}")
                 nc.tensor.matmul_mx(
-                    out=banks[m],
+                    out=bank[:],
                     lhsT=w2_codes[:, 2 * P * m : 2 * P * (m + 1)].bitcast(FP4X4),
                     lhsT_scale=w2_plane[:, P * m : P * (m + 1)],
                     rhs=z_codes[c][:].bitcast(FP8X4),
@@ -188,21 +182,24 @@ def tile_picked_deepset_none_p_kernel(tc, x_words, x_scales, w1, w2_words, w2_sc
                     start=True,
                     stop=True,
                 )
-            if last:
-                low = sb.tile([P, PIECE], F32, name="low")
-                high = sb.tile([P, PIECE], F32, name="high")
-                nc.scalar.copy(out=low[:], in_=banks[0])
-                nc.scalar.dma_start(out=out_view[:, 0, cols], in_=low[:])
-                nc.vector.tensor_copy(out=high[:], in_=banks[1])
-                nc.sync.dma_start(out=out_view[:, 1, cols], in_=high[:])
-            else:
-                result = sb.tile([P, N // P, PIECE], F32, name=f"result{c}")
-                nc.scalar.copy(out=result[:], in_=bank[:])
+                if m == 0 or c == 0:
+                    nc.scalar.copy(out=result[:, m, :], in_=bank[:])
+                else:
+                    nc.vector.tensor_copy(out=result[:, m, :], in_=bank[:])
+                if c == 0:
+                    nc.sync.dma_start(out=out_view[:, m, cols], in_=result[:, m, :])
+            if c == pieces - 1:
+                nc.scalar.dma_start(out=out_view[:, 0, cols], in_=result[:, 0, :])
+                nc.sync.dma_start(out=out_view[:, 1, cols], in_=result[:, 1, :])
+            elif c > 0:
                 nc.sync.dma_start(out=out_view[:, :, cols], in_=result[:])
 
-        weave(0, False)
-        weave(1, False)
-        weave(2, True)
-        weave(3, True)
-        for c in range(pieces):
-            second_product(c)
+        weave(0, 0, PIECE, False)
+        weave(1, 0, PIECE, False)
+        weave(2, 0, PIECE, True)
+        second_product(0)
+        weave(3, 0, PIECE // 2, True)
+        weave(3, PIECE // 2, PIECE, False)
+        second_product(1)
+        second_product(2)
+        second_product(3)

@@ -45,7 +45,7 @@ def tile_picked_deepset_none_p_kernel(tc, x_words, x_scales, w1, w2_words, w2_sc
         nc.vector.memset(xs_table[:].bitcast(I32), 0)
         nc.vector.memset(w2_plane[:].bitcast(I32), 0)
         w1_rows = w1.rearrange("(p j) c -> p j c", j=PACK)
-        nc.sync.dma_start(out=w1_raw[0][:], in_=w1_rows[:, :, : H // 2])
+        nc.scalar.dma_start(out=w1_raw[0][:], in_=w1_rows[:, :, : H // 2])
         nc.sync.dma_start(offsets[:], offs)
         load_scale_rows(nc.sync, xs_table, x_scales[0])
         nc.sync.dma_start(out=w1_raw[1][:], in_=w1_rows[:, :, H // 2 :])

@@ -36,7 +36,7 @@ def tile_picked_deepset_none_p_kernel(tc, x_words, x_scales, w1, w2_words, w2_sc
         ps = ctx.enter_context(tc.psum_pool(name="ps", bufs=1))
 
         offsets = sb.tile([P, S // 16], U16, name="offsets")
-        x_table = sb.tile([P, T], I32, name="x_table", tag="x_table", align_bytes=64)
+        x_table = sb.tile([P, T], I32, name="x_table", align_bytes=64)
         xs_table = sb.tile([P, T], U8, name="xs_table", align_bytes=64)
         w1_raw = [sb.tile([P, PACK, H // 2], F32, name=f"w1_raw{u}", align_bytes=64) for u in range(2)]
         w2_codes = sb.tile([P, 2 * N], U8, name="w2_codes", align_bytes=64)
@@ -45,110 +45,84 @@ def tile_picked_deepset_none_p_kernel(tc, x_words, x_scales, w1, w2_words, w2_sc
         nc.vector.memset(xs_table[:].bitcast(I32), 0)
         nc.vector.memset(w2_plane[:].bitcast(I32), 0)
         w1_rows = w1.rearrange("(p j) c -> p j c", j=PACK)
-        nc.scalar.dma_start(out=w1_raw[0][:], in_=w1_rows[:, :, : H // 2])
+        nc.sync.dma_start(out=x_table[:], in_=x_words[0].rearrange("p n r -> p (n r)").bitcast(I32))
         nc.sync.dma_start(offsets[:], offs)
         load_scale_rows(nc.sync, xs_table, x_scales[0])
-        nc.sync.dma_start(out=w1_raw[1][:], in_=w1_rows[:, :, H // 2 :])
-        nc.sync.dma_start(out=x_table[:], in_=x_words[0].rearrange("p n r -> p (n r)").bitcast(I32))
+        for u in range(2):
+            nc.sync.dma_start(out=w1_raw[u][:], in_=w1_rows[:, :, u * H // 2 : (u + 1) * H // 2])
         nc.sync.dma_start(out=w2_codes[:].bitcast(I32), in_=w2_words[0].bitcast(I32))
         load_scale_rows(nc.sync, w2_plane, w2_scales[0])
 
+        x_picked = sb.tile([P, S], U32, name="x_picked", align_bytes=64)
         xs_picked = sb.tile([P, S], U8, name="xs_picked", align_bytes=64)
+        nc.vector.tensor_copy(x_picked[:], x_table[:].bitcast(U32).indirect(offsets[:]))
         nc.vector.tensor_copy(xs_picked[:], xs_table[:].indirect(offsets[:]))
 
         w1_src = [tile[:].rearrange("p j (m t) -> p m j t", t=PACK) for tile in w1_raw]
         w1_bf = [sb.tile([P, 2, P, PACK], BF16, name=f"w1_bf{u}", align_bytes=64) for u in range(2)]
-        w1_codes = [sb.tile([P, 2 * P], U32, name="early_codes", align_bytes=64)]
-        w1_plane = [sb.tile([P, 2 * P], U8, name=f"w1_plane{u}", align_bytes=64) for u in range(2)]
+        w1_codes = [sb.tile([P, P], U32, name=f"w1_codes{t}", align_bytes=64) for t in range(PACK)]
+        w1_plane = [sb.tile([P, P], U8, name=f"w1_plane{t}", align_bytes=64) for t in range(PACK)]
         w1_dst = [tile[:].rearrange("p t m j -> p m j t") for tile in w1_bf]
-        low_m, high_m = slice(0, P // 2), slice(P // 2, P)
-        nc.scalar.activation(out=w1_dst[0][:, low_m], in_=w1_src[0][:, :, :, 0:2], func=COPY)
-        nc.scalar.activation(out=w1_dst[1][:, low_m], in_=w1_src[0][:, :, :, 2:4], func=COPY)
-        nc.vector.tensor_copy(out=w1_dst[0][:, high_m], in_=w1_src[1][:, :, :, 0:2])
-        nc.scalar.activation(out=w1_dst[1][:, high_m], in_=w1_src[1][:, :, :, 2:4], func=COPY)
-
-        def quantize_w1(u):
+        low_m = slice(0, P // 2)
+        share = 40
+        for u in range(2):
+            nc.scalar.activation(out=w1_dst[u][:, low_m], in_=w1_src[0][:, :, :, 2 * u : 2 * u + 2], func=COPY)
+        for u in range(2):
+            nc.vector.tensor_copy(out=w1_dst[u][:, P // 2 : P // 2 + share], in_=w1_src[1][:, :share, :, 2 * u : 2 * u + 2])
+            nc.scalar.activation(out=w1_dst[u][:, P // 2 + share :], in_=w1_src[1][:, share:, :, 2 * u : 2 * u + 2], func=COPY)
+        for t in range(PACK):
             nc.vector.quantize_mx(
-                out=w1_codes[u][:].bitcast(FP8X4),
-                scales=w1_plane[u][:],
-                in_=w1_bf[u][:].rearrange("p t m j -> p (t m j)"),
+                out=w1_codes[t][:].bitcast(FP8X4),
+                scales=w1_plane[t][:],
+                in_=w1_bf[t // 2][:, t % 2].rearrange("p m j -> p (m j)"),
             )
-
-        quantize_w1(0)
-
-        pieces = S // PIECE
-        x_picked = sb.tile([P, S], U32, name="x_picked", align_bytes=64)
-        for c in range(pieces):
-            nc.vector.tensor_copy(
-                x_picked[:, c * PIECE : (c + 1) * PIECE],
-                x_table[:].bitcast(U32).indirect(offsets[:, c * PIECE // 16 : (c + 1) * PIECE // 16]),
-            )
-        w1_codes.append(sb.tile([P, 2 * P], U32, name="late_codes", tag="x_table", align_bytes=64))
-        quantize_w1(1)
 
         scaled = [sb.tile([P, S], F32, name=f"scaled{t}", align_bytes=64) for t in range(PACK)]
-        partial = [sb.tile([P, 1], F32, name=f"partial{t}") for t in range(2)]
         neg_mean = [sb.tile([P, 1], F32, name=f"neg_mean{t}") for t in range(PACK)]
         planes = [sb.tile([P, PACK, HALF], BF16, name=f"planes{a}", align_bytes=64) for a in range(2)]
-        split = (HALF, S - PIECE, S, S)
-        front_bank = [ps.tile([P, split[t]], F32, name=f"front{t}", tag=f"bank{t}") for t in range(PACK)]
-        back_bank = [ps.tile([P, S - split[t]], F32, name=f"back{t}", tag=f"bank{PACK + t}") for t in range(2)]
 
-        def first_product(t, start, width):
-            group = slice((t % 2) * P, (t % 2 + 1) * P)
-            cols = slice(start, start + width)
-            bank = front_bank[t][:, cols] if start < split[t] else back_bank[t][:, start - split[t] : start - split[t] + width]
+        def first_product(t, cols, bank_no):
+            bank = ps.tile([P, cols.stop - cols.start], F32, name=f"h{bank_no}", tag=f"bank{bank_no}")
             nc.tensor.matmul_mx(
-                out=bank,
-                lhsT=w1_codes[t // 2][:, group].bitcast(FP8X4),
-                lhsT_scale=w1_plane[t // 2][:, group],
+                out=bank[:],
+                lhsT=w1_codes[t][:].bitcast(FP8X4),
+                lhsT_scale=w1_plane[t][:],
                 rhs=x_picked[:, cols].bitcast(FP8X4),
                 rhs_scale=xs_picked[:, cols],
                 start=True,
                 stop=True,
             )
+            return bank
 
-        def empty_front(t):
-            total = partial[t] if split[t] < S else neg_mean[t]
-            nc.scalar.activation(out=scaled[t][:, : split[t]], in_=front_bank[t][:], func=COPY, scale=-1.0 / S, accum_out=total[:])
+        def empty_scalar(t, cols, bank, total):
+            nc.scalar.activation(out=scaled[t][:, cols], in_=bank[:], func=COPY, scale=-1.0 / S, accum_out=total)
 
-        def empty_back(t):
+        def empty_vector(t, cols, bank, first, total):
+            nc.vector.tensor_scalar(out=scaled[t][:, cols], in0=bank[:], scalar1=-1.0 / S, scalar2=first, op0=MULT, op1=ADD, accum_out=total)
+
+        def centre(t, a):
             nc.vector.tensor_scalar(
-                out=scaled[t][:, split[t] :],
-                in0=back_bank[t][:],
-                scalar1=-1.0 / S,
-                scalar2=partial[t][:],
-                op0=MULT,
-                op1=ADD,
-                accum_out=neg_mean[t][:],
+                out=planes[a][:, t, :], in0=scaled[t][:, a * HALF : (a + 1) * HALF], scalar1=-float(S), scalar2=neg_mean[t][:], op0=MULT, op1=ADD
             )
 
-        def centre(t, start, width, on_scalar):
-            dst = planes[start // HALF][:, t, start % HALF : start % HALF + width]
-            src = scaled[t][:, start : start + width]
-            if not on_scalar:
-                nc.vector.tensor_scalar(out=dst, in0=src, scalar1=-float(S), scalar2=neg_mean[t][:], op0=MULT, op1=ADD)
-            else:
-                nc.scalar.activation(out=dst, in_=src, func=IDENT, scale=-float(S), bias=neg_mean[t][:])
+        front, back, both = slice(0, HALF), slice(HALF, S), slice(0, S)
+        def centre_scalar(t, a):
+            nc.scalar.activation(
+                out=planes[a][:, t, :], in_=scaled[t][:, a * HALF : (a + 1) * HALF], func=IDENT, scale=-float(S), bias=neg_mean[t][:]
+            )
 
-        for c in range(pieces):
-            for t in range(2):
-                first_product(t, c * PIECE, PIECE)
-        for t in range(2, PACK):
-            for a in range(2):
-                first_product(t, a * HALF, HALF)
-        for t in range(PACK):
-            empty_front(t)
-        for t in range(2):
-            empty_back(t)
-        for t in range(2):
-            centre(t, 0, HALF, False)
-            centre(t, HALF, HALF, False)
-        centre(2, 0, HALF, False)
-        centre(2, HALF, HALF, False)
-        centre(3, 0, HALF, False)
-        centre(3, HALF, HALF, False)
+        banks = [first_product(t, both, t) for t in range(PACK)]
+        empty_vector(0, both, banks[0], None, neg_mean[0][:])
+        empty_scalar(1, both, banks[1], neg_mean[1][:])
+        centre(0, 0)
+        centre_scalar(0, 1)
+        empty_vector(2, both, banks[2], None, neg_mean[2][:])
+        empty_scalar(3, both, banks[3], neg_mean[3][:])
+        for t in range(1, PACK):
+            centre(t, 0)
+            centre(t, 1)
 
+        pieces = S // PIECE
         z_bf = [sb.tile([P, PIECE, PACK], BF16, name=f"z_bf{c}", align_bytes=64) for c in range(pieces)]
         z_codes = [sb.tile([P, PIECE], U32, name=f"z_codes{c}", align_bytes=64) for c in range(pieces)]
         z_plane = [sb.tile([P, PIECE], U8, name=f"z_plane{c}", align_bytes=64) for c in range(pieces)]
@@ -188,10 +162,7 @@ def tile_picked_deepset_none_p_kernel(tc, x_words, x_scales, w1, w2_words, w2_sc
                     nc.vector.tensor_copy(out=result[:, m, :], in_=bank[:])
                 if c == 0:
                     nc.sync.dma_start(out=out_view[:, m, cols], in_=result[:, m, :])
-            if c == pieces - 1:
-                nc.scalar.dma_start(out=out_view[:, 0, cols], in_=result[:, 0, :])
-                nc.sync.dma_start(out=out_view[:, 1, cols], in_=result[:, 1, :])
-            elif c > 0:
+            if c > 0:
                 nc.sync.dma_start(out=out_view[:, :, cols], in_=result[:])
 
         weave(0, 0, PIECE, False)

@@ -118,7 +118,9 @@ def tile_picked_deepset_none_p_kernel(tc, x_words, x_scales, w1, w2_words, w2_sc
         centre_scalar(0, 1)
         empty_vector(2, both, banks[2], None, neg_mean[2][:])
         empty_scalar(3, both, banks[3], neg_mean[3][:])
-        for t in range(1, PACK):
+        centre(1, 0)
+        centre_scalar(1, 1)
+        for t in range(2, PACK):
             centre(t, 0)
             centre(t, 1)
 
@@ -165,12 +167,14 @@ def tile_picked_deepset_none_p_kernel(tc, x_words, x_scales, w1, w2_words, w2_sc
             if c > 0:
                 nc.sync.dma_start(out=out_view[:, :, cols], in_=result[:])
 
-        weave(0, 0, PIECE, False)
-        weave(1, 0, PIECE, False)
-        weave(2, 0, PIECE, True)
-        second_product(0)
-        weave(3, 0, PIECE // 2, True)
-        weave(3, PIECE // 2, PIECE, False)
-        second_product(1)
-        second_product(2)
-        second_product(3)
+        vector_share = (80, 80, 64, 64)
+
+        def weave_shared(c):
+            weave(c, 0, vector_share[c], False)
+            weave(c, vector_share[c], PIECE, True)
+
+        weave_shared(0)
+        for c in range(pieces):
+            if c + 1 < pieces:
+                weave_shared(c + 1)
+            second_product(c)

@@ -16,7 +16,6 @@ FP4X4 = mybir.dt.float4_e2m1fn_x4
 MULT = mybir.AluOpType.mult
 ADD = mybir.AluOpType.add
 COPY = mybir.ActivationFunctionType.Copy
-IDENT = mybir.ActivationFunctionType.Identity
 
 P = 128
 PACK = 4
@@ -58,6 +57,21 @@ def tile_picked_deepset_none_p_kernel(tc, x_words, x_scales, w1, w2_words, w2_sc
         nc.vector.tensor_copy(x_picked[:], x_table[:].bitcast(U32).indirect(offsets[:]))
         nc.vector.tensor_copy(xs_picked[:], xs_table[:].indirect(offsets[:]))
 
+        warm = ps.tile([P // 2, S], F32, name="warm", tag="bank7")
+
+        def warm_up(codes, plane):
+            nc.tensor.matmul_mx(
+                out=warm[:],
+                lhsT=codes[:, : P // 2].bitcast(FP8X4),
+                lhsT_scale=plane[:, : P // 2],
+                rhs=x_picked[:].bitcast(FP8X4),
+                rhs_scale=xs_picked[:],
+                start=True,
+                stop=True,
+            )
+
+        warm_up(x_picked, xs_picked)
+
         w1_src = [tile[:].rearrange("p j (m t) -> p m j t", t=PACK) for tile in w1_raw]
         w1_bf = [sb.tile([P, 2, P, PACK], BF16, name=f"w1_bf{u}", align_bytes=64) for u in range(2)]
         w1_codes = [sb.tile([P, P], U32, name=f"w1_codes{t}", align_bytes=64) for t in range(PACK)]
@@ -79,72 +93,57 @@ def tile_picked_deepset_none_p_kernel(tc, x_words, x_scales, w1, w2_words, w2_sc
 
         scaled = [sb.tile([P, S], F32, name=f"scaled{t}", align_bytes=64) for t in range(PACK)]
         neg_mean = [sb.tile([P, 1], F32, name=f"neg_mean{t}") for t in range(PACK)]
-        planes = [sb.tile([P, PACK, HALF], BF16, name=f"planes{a}", align_bytes=64) for a in range(2)]
+        pairs = sb.tile([P, 2, S, 2], BF16, name="pairs", align_bytes=64)
 
-        def first_product(t, cols, bank_no):
-            bank = ps.tile([P, cols.stop - cols.start], F32, name=f"h{bank_no}", tag=f"bank{bank_no}")
-            nc.tensor.matmul_mx(
-                out=bank[:],
-                lhsT=w1_codes[t][:].bitcast(FP8X4),
-                lhsT_scale=w1_plane[t][:],
-                rhs=x_picked[:, cols].bitcast(FP8X4),
-                rhs_scale=xs_picked[:, cols],
-                start=True,
-                stop=True,
-            )
+        def first_product(t):
+            bank = ps.tile([P, S], F32, name=f"h{t}", tag=f"bank{t}")
+            width = HALF if t < 2 else PIECE
+            for lo in range(0, S, width):
+                nc.tensor.matmul_mx(
+                    out=bank[:, lo : lo + width],
+                    lhsT=w1_codes[t][:].bitcast(FP8X4),
+                    lhsT_scale=w1_plane[t][:],
+                    rhs=x_picked[:, lo : lo + width].bitcast(FP8X4),
+                    rhs_scale=xs_picked[:, lo : lo + width],
+                    start=True,
+                    stop=True,
+                )
             return bank
 
-        def empty_scalar(t, cols, bank, total):
-            nc.scalar.activation(out=scaled[t][:, cols], in_=bank[:], func=COPY, scale=-1.0 / S, accum_out=total)
+        def empty_scalar(t, bank):
+            nc.scalar.activation(out=scaled[t][:], in_=bank[:], func=COPY, scale=-1.0 / S, accum_out=neg_mean[t][:])
 
-        def empty_vector(t, cols, bank, first, total):
-            nc.vector.tensor_scalar(out=scaled[t][:, cols], in0=bank[:], scalar1=-1.0 / S, scalar2=first, op0=MULT, op1=ADD, accum_out=total)
+        def empty_vector(t, bank):
+            nc.vector.tensor_scalar(out=scaled[t][:], in0=bank[:], scalar1=-1.0 / S, scalar2=None, op0=MULT, op1=ADD, accum_out=neg_mean[t][:])
 
-        def centre(t, a):
+        def centre(t, lo, hi):
             nc.vector.tensor_scalar(
-                out=planes[a][:, t, :], in0=scaled[t][:, a * HALF : (a + 1) * HALF], scalar1=-float(S), scalar2=neg_mean[t][:], op0=MULT, op1=ADD
+                out=pairs[:, t // 2, lo:hi, t % 2], in0=scaled[t][:, lo:hi], scalar1=-float(S), scalar2=neg_mean[t][:], op0=MULT, op1=ADD
             )
-
-        front, back, both = slice(0, HALF), slice(HALF, S), slice(0, S)
-        def centre_scalar(t, a):
-            nc.scalar.activation(
-                out=planes[a][:, t, :], in_=scaled[t][:, a * HALF : (a + 1) * HALF], func=IDENT, scale=-float(S), bias=neg_mean[t][:]
-            )
-
-        banks = [first_product(t, both, t) for t in range(PACK)]
-        empty_vector(0, both, banks[0], None, neg_mean[0][:])
-        empty_scalar(1, both, banks[1], neg_mean[1][:])
-        centre(0, 0)
-        centre_scalar(0, 1)
-        empty_vector(2, both, banks[2], None, neg_mean[2][:])
-        empty_scalar(3, both, banks[3], neg_mean[3][:])
-        centre(1, 0)
-        centre_scalar(1, 1)
-        for t in range(2, PACK):
-            centre(t, 0)
-            centre(t, 1)
 
         pieces = S // PIECE
         z_bf = [sb.tile([P, PIECE, PACK], BF16, name=f"z_bf{c}", align_bytes=64) for c in range(pieces)]
         z_codes = [sb.tile([P, PIECE], U32, name=f"z_codes{c}", align_bytes=64) for c in range(pieces)]
         z_plane = [sb.tile([P, PIECE], U8, name=f"z_plane{c}", align_bytes=64) for c in range(pieces)]
         out_view = out.rearrange("(m p) n -> p m n", p=P)
+        words = pairs[:].rearrange("p u n e -> p u (n e)").bitcast(U32)
 
-        def weave(c, lo, hi, on_scalar):
-            start = (c % 2) * PIECE
-            src = planes[c // 2][:, :, start + lo : start + hi].rearrange("p t (n i) -> p n t i", i=PACK)
-            dst = z_bf[c][:, lo:hi, :].rearrange("p (n i) t -> p n t i", i=PACK)
+        def weave(c, on_scalar):
+            src = words[:, :, c * PIECE : (c + 1) * PIECE].rearrange("p u n -> p n u")
+            dst = z_bf[c][:].rearrange("p n t -> p (n t)").bitcast(U32).rearrange("p (n u) -> p n u", u=2)
             if on_scalar:
                 nc.scalar.copy(out=dst, in_=src)
             else:
-                nc.vector.tensor_copy(out=dst, in_=src)
+                nc.vector.tensor_copy(out=dst.bitcast(I32), in_=src.bitcast(I32))
 
-        def second_product(c):
+        def quantise(c):
             nc.vector.quantize_mx(
                 out=z_codes[c][:].bitcast(FP8X4),
                 scales=z_plane[c][:],
                 in_=z_bf[c][:].rearrange("p n t -> p (n t)"),
             )
+
+        def second_product(c):
             cols = slice(c * PIECE, (c + 1) * PIECE)
             result = sb.tile([P, N // P, PIECE], F32, name=f"result{c}", align_bytes=64)
             for m in range(N // P):
@@ -158,7 +157,7 @@ def tile_picked_deepset_none_p_kernel(tc, x_words, x_scales, w1, w2_words, w2_sc
                     start=True,
                     stop=True,
                 )
-                if m == 0 or c == 0:
+                if m == 0:
                     nc.scalar.copy(out=result[:, m, :], in_=bank[:])
                 else:
                     nc.vector.tensor_copy(out=result[:, m, :], in_=bank[:])
@@ -167,14 +166,23 @@ def tile_picked_deepset_none_p_kernel(tc, x_words, x_scales, w1, w2_words, w2_sc
             if c > 0:
                 nc.sync.dma_start(out=out_view[:, :, cols], in_=result[:])
 
-        vector_share = (80, 80, 64, 64)
-
-        def weave_shared(c):
-            weave(c, 0, vector_share[c], False)
-            weave(c, vector_share[c], PIECE, True)
-
-        weave_shared(0)
+        banks = [first_product(t) for t in range(PACK)]
+        warm_up(w1_codes[3], w1_plane[3])
+        empty_scalar(0, banks[0])
+        empty_vector(1, banks[1])
+        empty_scalar(2, banks[2])
+        empty_scalar(3, banks[3])
+        for t in range(PACK - 1):
+            centre(t, 0, S)
+        centre(3, 0, PIECE)
+        centre(3, PIECE, HALF)
+        weave(0, False)
+        centre(3, HALF, S)
+        quantise(0)
+        weave(1, False)
+        weave(2, True)
+        weave(3, True)
+        for c in range(1, pieces):
+            quantise(c)
         for c in range(pieces):
-            if c + 1 < pieces:
-                weave_shared(c + 1)
             second_product(c)

@@ -16,6 +16,7 @@ FP4X4 = mybir.dt.float4_e2m1fn_x4
 MULT = mybir.AluOpType.mult
 ADD = mybir.AluOpType.add
 COPY = mybir.ActivationFunctionType.Copy
+IDENT = mybir.ActivationFunctionType.Identity
 
 P = 128
 PACK = 4
@@ -57,21 +58,6 @@ def tile_picked_deepset_none_p_kernel(tc, x_words, x_scales, w1, w2_words, w2_sc
         nc.vector.tensor_copy(x_picked[:], x_table[:].bitcast(U32).indirect(offsets[:]))
         nc.vector.tensor_copy(xs_picked[:], xs_table[:].indirect(offsets[:]))
 
-        warm = ps.tile([P // 2, S], F32, name="warm", tag="bank7")
-
-        def warm_up(codes, plane):
-            nc.tensor.matmul_mx(
-                out=warm[:],
-                lhsT=codes[:, : P // 2].bitcast(FP8X4),
-                lhsT_scale=plane[:, : P // 2],
-                rhs=x_picked[:].bitcast(FP8X4),
-                rhs_scale=xs_picked[:],
-                start=True,
-                stop=True,
-            )
-
-        warm_up(x_picked, xs_picked)
-
         w1_src = [tile[:].rearrange("p j (m t) -> p m j t", t=PACK) for tile in w1_raw]
         w1_bf = [sb.tile([P, 2, P, PACK], BF16, name=f"w1_bf{u}", align_bytes=64) for u in range(2)]
         w1_codes = [sb.tile([P, P], U32, name=f"w1_codes{t}", align_bytes=64) for t in range(PACK)]
@@ -79,57 +65,77 @@ def tile_picked_deepset_none_p_kernel(tc, x_words, x_scales, w1, w2_words, w2_sc
         w1_dst = [tile[:].rearrange("p t m j -> p m j t") for tile in w1_bf]
         low_m = slice(0, P // 2)
         share = 40
-        for u in range(2):
+        for u in (1, 0):
             nc.scalar.activation(out=w1_dst[u][:, low_m], in_=w1_src[0][:, :, :, 2 * u : 2 * u + 2], func=COPY)
-        for u in range(2):
+        for u in (1, 0):
             nc.vector.tensor_copy(out=w1_dst[u][:, P // 2 : P // 2 + share], in_=w1_src[1][:, :share, :, 2 * u : 2 * u + 2])
             nc.scalar.activation(out=w1_dst[u][:, P // 2 + share :], in_=w1_src[1][:, share:, :, 2 * u : 2 * u + 2], func=COPY)
-        for t in range(PACK):
+        for t in (2, 0, 1, 3):
             nc.vector.quantize_mx(
                 out=w1_codes[t][:].bitcast(FP8X4),
                 scales=w1_plane[t][:],
                 in_=w1_bf[t // 2][:, t % 2].rearrange("p m j -> p (m j)"),
             )
 
-        scaled = [sb.tile([P, S], F32, name=f"scaled{t}", align_bytes=64) for t in range(PACK)]
+        pieces = S // PIECE
+        last = PACK - 1
+        scaled = [sb.tile([P, S], F32, name=f"scaled{t}", align_bytes=64) for t in range(last)]
+        folded = sb.tile([P, PIECE], F32, name="folded", align_bytes=64)
         neg_mean = [sb.tile([P, 1], F32, name=f"neg_mean{t}") for t in range(PACK)]
-        pairs = sb.tile([P, 2, S, 2], BF16, name="pairs", align_bytes=64)
+        spans = ((0, PIECE), (PIECE, S))
+        pairs = [sb.tile([P, 2, hi - lo, 2], BF16, name=f"pairs{lo}", align_bytes=64) for lo, hi in spans]
 
-        def first_product(t):
-            bank = ps.tile([P, S], F32, name=f"h{t}", tag=f"bank{t}")
-            width = HALF if t < 2 else PIECE
-            for lo in range(0, S, width):
-                nc.tensor.matmul_mx(
-                    out=bank[:, lo : lo + width],
-                    lhsT=w1_codes[t][:].bitcast(FP8X4),
-                    lhsT_scale=w1_plane[t][:],
-                    rhs=x_picked[:, lo : lo + width].bitcast(FP8X4),
-                    rhs_scale=xs_picked[:, lo : lo + width],
-                    start=True,
-                    stop=True,
-                )
-            return bank
-
-        def empty_scalar(t, bank):
-            nc.scalar.activation(out=scaled[t][:], in_=bank[:], func=COPY, scale=-1.0 / S, accum_out=neg_mean[t][:])
-
-        def empty_vector(t, bank):
-            nc.vector.tensor_scalar(out=scaled[t][:], in0=bank[:], scalar1=-1.0 / S, scalar2=None, op0=MULT, op1=ADD, accum_out=neg_mean[t][:])
-
-        def centre(t, lo, hi):
-            nc.vector.tensor_scalar(
-                out=pairs[:, t // 2, lo:hi, t % 2], in0=scaled[t][:, lo:hi], scalar1=-float(S), scalar2=neg_mean[t][:], op0=MULT, op1=ADD
+        def first_pass(t, dst, lo, hi, start=True, stop=True):
+            nc.tensor.matmul_mx(
+                out=dst,
+                lhsT=w1_codes[t][:].bitcast(FP8X4),
+                lhsT_scale=w1_plane[t][:],
+                rhs=x_picked[:, lo:hi].bitcast(FP8X4),
+                rhs_scale=xs_picked[:, lo:hi],
+                start=start,
+                stop=stop,
             )
 
-        pieces = S // PIECE
+        banks = [ps.tile([P, S], F32, name=f"h{t}", tag=f"bank{t}") for t in range(last)]
+        for t in (2, 0, 1):
+            first_pass(t, banks[t][:], 0, S)
+        fold = ps.tile([P, PIECE], F32, name="fold", tag="bank3")
+        for c in range(pieces):
+            first_pass(last, fold[:], c * PIECE, (c + 1) * PIECE, c == 0, c == pieces - 1)
+        tail_spans = ((0, PIECE), (PIECE, HALF), (HALF, S))
+        tails = [ps.tile([P, hi - lo], F32, name=f"tail{lo}", tag=f"bank{4 + a}") for a, (lo, hi) in enumerate(tail_spans)]
+        for a, (lo, hi) in enumerate(tail_spans):
+            first_pass(last, tails[a][:], lo, hi)
+
+        def empty(src, dst, total, on_scalar):
+            if on_scalar:
+                nc.scalar.activation(out=dst, in_=src, func=COPY, scale=-1.0 / S, accum_out=total)
+            else:
+                nc.vector.tensor_scalar(out=dst, in0=src, scalar1=-1.0 / S, scalar2=None, op0=MULT, op1=ADD, accum_out=total)
+
+        def centre(t, lo, hi, on_scalar=False):
+            a = max(i for i, span in enumerate(spans) if span[0] <= lo)
+            dst = pairs[a][:, t // 2, lo - spans[a][0] : hi - spans[a][0], t % 2]
+            if t == last:
+                b = max(i for i, span in enumerate(tail_spans) if span[0] <= lo)
+                src, factor = tails[b][:, lo - tail_spans[b][0] : hi - tail_spans[b][0]], 1.0
+            else:
+                src, factor = scaled[t][:, lo:hi], -float(S)
+            if on_scalar:
+                nc.scalar.activation(out=dst, in_=src, func=IDENT, scale=factor, bias=neg_mean[t][:])
+            else:
+                nc.vector.tensor_scalar(out=dst, in0=src, scalar1=factor, scalar2=neg_mean[t][:], op0=MULT, op1=ADD)
+
         z_bf = [sb.tile([P, PIECE, PACK], BF16, name=f"z_bf{c}", align_bytes=64) for c in range(pieces)]
         z_codes = [sb.tile([P, PIECE], U32, name=f"z_codes{c}", align_bytes=64) for c in range(pieces)]
         z_plane = [sb.tile([P, PIECE], U8, name=f"z_plane{c}", align_bytes=64) for c in range(pieces)]
         out_view = out.rearrange("(m p) n -> p m n", p=P)
-        words = pairs[:].rearrange("p u n e -> p u (n e)").bitcast(U32)
 
         def weave(c, on_scalar):
-            src = words[:, :, c * PIECE : (c + 1) * PIECE].rearrange("p u n -> p n u")
+            a = max(i for i, span in enumerate(spans) if span[0] <= c * PIECE)
+            start = c * PIECE - spans[a][0]
+            words = pairs[a][:].rearrange("p u n e -> p u (n e)").bitcast(U32)
+            src = words[:, :, start : start + PIECE].rearrange("p u n -> p n u")
             dst = z_bf[c][:].rearrange("p n t -> p (n t)").bitcast(U32).rearrange("p (n u) -> p n u", u=2)
             if on_scalar:
                 nc.scalar.copy(out=dst, in_=src)
@@ -157,7 +163,7 @@ def tile_picked_deepset_none_p_kernel(tc, x_words, x_scales, w1, w2_words, w2_sc
                     start=True,
                     stop=True,
                 )
-                if m == 0:
+                if m == 0 or c == 0:
                     nc.scalar.copy(out=result[:, m, :], in_=bank[:])
                 else:
                     nc.vector.tensor_copy(out=result[:, m, :], in_=bank[:])
@@ -166,23 +172,22 @@ def tile_picked_deepset_none_p_kernel(tc, x_words, x_scales, w1, w2_words, w2_sc
             if c > 0:
                 nc.sync.dma_start(out=out_view[:, :, cols], in_=result[:])
 
-        banks = [first_product(t) for t in range(PACK)]
-        warm_up(w1_codes[3], w1_plane[3])
-        empty_scalar(0, banks[0])
-        empty_vector(1, banks[1])
-        empty_scalar(2, banks[2])
-        empty_scalar(3, banks[3])
-        for t in range(PACK - 1):
-            centre(t, 0, S)
-        centre(3, 0, PIECE)
-        centre(3, PIECE, HALF)
+        empty(banks[2][:], scaled[2][:], neg_mean[2][:], False)
+        empty(banks[0][:], scaled[0][:], neg_mean[0][:], True)
+        empty(banks[1][:], scaled[1][:], neg_mean[1][:], True)
+        for lo, hi in spans:
+            centre(2, lo, hi)
+        centre(0, 0, PIECE)
+        empty(fold[:], folded[:], neg_mean[last][:], False)
+        for lo, hi in tail_spans:
+            centre(last, lo, hi, True)
+        centre(1, 0, PIECE)
         weave(0, False)
-        centre(3, HALF, S)
         quantise(0)
-        weave(1, False)
-        weave(2, True)
-        weave(3, True)
+        for t in range(2):
+            centre(t, PIECE, S)
         for c in range(1, pieces):
+            weave(c, c > 1)
             quantise(c)
         for c in range(pieces):
             second_product(c)

@@ -107,6 +107,17 @@ def tile_picked_deepset_none_p_kernel(tc, x_words, x_scales, w1, w2_words, w2_sc
         for a, (lo, hi) in enumerate(tail_spans):
             first_pass(last, tails[a][:], lo, hi)
 
+        warm = ps.tile([64, S], F32, name="warm", tag="bank7")
+        nc.tensor.matmul_mx(
+            out=warm[:],
+            lhsT=w1_codes[last][:, :64].bitcast(FP8X4),
+            lhsT_scale=w1_plane[last][:, :64],
+            rhs=x_picked[:].bitcast(FP8X4),
+            rhs_scale=xs_picked[:],
+            start=True,
+            stop=True,
+        )
+
         def empty(src, dst, total, on_scalar):
             if on_scalar:
                 nc.scalar.activation(out=dst, in_=src, func=COPY, scale=-1.0 / S, accum_out=total)

@@ -82,8 +82,9 @@ def tile_picked_deepset_none_p_kernel(tc, x_words, x_scales, w1, w2_words, w2_sc
         scaled = [sb.tile([P, S], F32, name=f"scaled{t}", align_bytes=64) for t in range(last)]
         folded = sb.tile([P, PIECE], F32, name="folded", align_bytes=64)
         neg_mean = [sb.tile([P, 1], F32, name=f"neg_mean{t}") for t in range(PACK)]
-        spans = ((0, PIECE), (PIECE, S))
-        pairs = [sb.tile([P, 2, hi - lo, 2], BF16, name=f"pairs{lo}", align_bytes=64) for lo, hi in spans]
+        pair_row = sb.tile([P, PACK * S], BF16, name="pair_row", align_bytes=64)
+        pairs = pair_row[:].rearrange("p (c u n e) -> p c u n e", u=2, n=PIECE, e=2)
+        pair_words = pair_row[:].bitcast(U32).rearrange("p (c u n) -> p c n u", u=2, n=PIECE)
 
         def first_pass(t, dst, lo, hi, start=True, stop=True):
             nc.tensor.matmul_mx(
@@ -102,7 +103,7 @@ def tile_picked_deepset_none_p_kernel(tc, x_words, x_scales, w1, w2_words, w2_sc
         fold = ps.tile([P, PIECE], F32, name="fold", tag="bank3")
         for c in range(pieces):
             first_pass(last, fold[:], c * PIECE, (c + 1) * PIECE, c == 0, c == pieces - 1)
-        tail_spans = ((0, PIECE), (PIECE, HALF), (HALF, S))
+        tail_spans = ((0, HALF), (HALF, S))
         tails = [ps.tile([P, hi - lo], F32, name=f"tail{lo}", tag=f"bank{4 + a}") for a, (lo, hi) in enumerate(tail_spans)]
         for a, (lo, hi) in enumerate(tail_spans):
             first_pass(last, tails[a][:], lo, hi)
@@ -125,13 +126,13 @@ def tile_picked_deepset_none_p_kernel(tc, x_words, x_scales, w1, w2_words, w2_sc
                 nc.vector.tensor_scalar(out=dst, in0=src, scalar1=-1.0 / S, scalar2=None, op0=MULT, op1=ADD, accum_out=total)
 
         def centre(t, lo, hi, on_scalar=False):
-            a = max(i for i, span in enumerate(spans) if span[0] <= lo)
-            dst = pairs[a][:, t // 2, lo - spans[a][0] : hi - spans[a][0], t % 2]
+            dst = pairs[:, lo // PIECE : hi // PIECE, t // 2, :, t % 2]
             if t == last:
                 b = max(i for i, span in enumerate(tail_spans) if span[0] <= lo)
                 src, factor = tails[b][:, lo - tail_spans[b][0] : hi - tail_spans[b][0]], 1.0
             else:
                 src, factor = scaled[t][:, lo:hi], -float(S)
+            src = src.rearrange("p (c n) -> p c n", n=PIECE)
             if on_scalar:
                 nc.scalar.activation(out=dst, in_=src, func=IDENT, scale=factor, bias=neg_mean[t][:])
             else:
@@ -143,10 +144,7 @@ def tile_picked_deepset_none_p_kernel(tc, x_words, x_scales, w1, w2_words, w2_sc
         out_view = out.rearrange("(m p) n -> p m n", p=P)
 
         def weave(c, on_scalar):
-            a = max(i for i, span in enumerate(spans) if span[0] <= c * PIECE)
-            start = c * PIECE - spans[a][0]
-            words = pairs[a][:].rearrange("p u n e -> p u (n e)").bitcast(U32)
-            src = words[:, :, start : start + PIECE].rearrange("p u n -> p n u")
+            src = pair_words[:, c]
             dst = z_bf[c][:].rearrange("p n t -> p (n t)").bitcast(U32).rearrange("p (n u) -> p n u", u=2)
             if on_scalar:
                 nc.scalar.copy(out=dst, in_=src)
@@ -186,19 +184,16 @@ def tile_picked_deepset_none_p_kernel(tc, x_words, x_scales, w1, w2_words, w2_sc
         empty(banks[2][:], scaled[2][:], neg_mean[2][:], False)
         empty(banks[0][:], scaled[0][:], neg_mean[0][:], True)
         empty(banks[1][:], scaled[1][:], neg_mean[1][:], True)
-        for lo, hi in spans:
-            centre(2, lo, hi)
-        centre(0, 0, PIECE)
+        centre(2, 0, S)
         empty(fold[:], folded[:], neg_mean[last][:], False)
         for lo, hi in tail_spans:
             centre(last, lo, hi, True)
-        centre(1, 0, PIECE)
-        weave(0, False)
-        quantise(0)
-        for t in range(2):
-            centre(t, PIECE, S)
-        for c in range(1, pieces):
+        centre(0, 0, S)
+        for lo, hi in tail_spans:
+            centre(1, lo, hi)
+        for c in range(pieces):
             weave(c, c > 1)
+        for c in range(pieces):
             quantise(c)
         for c in range(pieces):
             second_product(c)

@@ -103,21 +103,10 @@ def tile_picked_deepset_none_p_kernel(tc, x_words, x_scales, w1, w2_words, w2_sc
         fold = ps.tile([P, PIECE], F32, name="fold", tag="bank3")
         for c in range(pieces):
             first_pass(last, fold[:], c * PIECE, (c + 1) * PIECE, c == 0, c == pieces - 1)
-        tail_spans = ((0, HALF), (HALF, S))
+        tail_spans = tuple((c * PIECE, (c + 1) * PIECE) for c in range(pieces))
         tails = [ps.tile([P, hi - lo], F32, name=f"tail{lo}", tag=f"bank{4 + a}") for a, (lo, hi) in enumerate(tail_spans)]
         for a, (lo, hi) in enumerate(tail_spans):
             first_pass(last, tails[a][:], lo, hi)
-
-        warm = ps.tile([64, S], F32, name="warm", tag="bank7")
-        nc.tensor.matmul_mx(
-            out=warm[:],
-            lhsT=w1_codes[last][:, :64].bitcast(FP8X4),
-            lhsT_scale=w1_plane[last][:, :64],
-            rhs=x_picked[:].bitcast(FP8X4),
-            rhs_scale=xs_picked[:],
-            start=True,
-            stop=True,
-        )
 
         def empty(src, dst, total, on_scalar):
             if on_scalar:
@@ -126,13 +115,13 @@ def tile_picked_deepset_none_p_kernel(tc, x_words, x_scales, w1, w2_words, w2_sc
                 nc.vector.tensor_scalar(out=dst, in0=src, scalar1=-1.0 / S, scalar2=None, op0=MULT, op1=ADD, accum_out=total)
 
         def centre(t, lo, hi, on_scalar=False):
-            dst = pairs[:, lo // PIECE : hi // PIECE, t // 2, :, t % 2]
+            dst = pairs[:, lo // PIECE : hi // PIECE, t // 2, :, t % 2].rearrange("p c (h n) -> p h c n", h=2)
             if t == last:
                 b = max(i for i, span in enumerate(tail_spans) if span[0] <= lo)
                 src, factor = tails[b][:, lo - tail_spans[b][0] : hi - tail_spans[b][0]], 1.0
             else:
                 src, factor = scaled[t][:, lo:hi], -float(S)
-            src = src.rearrange("p (c n) -> p c n", n=PIECE)
+            src = src.rearrange("p (c h n) -> p h c n", h=2, n=PIECE // 2)
             if on_scalar:
                 nc.scalar.activation(out=dst, in_=src, func=IDENT, scale=factor, bias=neg_mean[t][:])
             else:
@@ -184,16 +173,31 @@ def tile_picked_deepset_none_p_kernel(tc, x_words, x_scales, w1, w2_words, w2_sc
         empty(banks[2][:], scaled[2][:], neg_mean[2][:], False)
         empty(banks[0][:], scaled[0][:], neg_mean[0][:], True)
         empty(banks[1][:], scaled[1][:], neg_mean[1][:], True)
+
+        warm = ps.tile([64, S], F32, name="warm", tag="bank2")
+        nc.tensor.matmul_mx(
+            out=warm[:],
+            lhsT=w1_codes[last][:, :64].bitcast(FP8X4),
+            lhsT_scale=w1_plane[last][:, :64],
+            rhs=x_picked[:].bitcast(FP8X4),
+            rhs_scale=xs_picked[:],
+            start=True,
+            stop=True,
+        )
         centre(2, 0, S)
+        centre(0, 0, PIECE)
         empty(fold[:], folded[:], neg_mean[last][:], False)
         for lo, hi in tail_spans:
             centre(last, lo, hi, True)
-        centre(0, 0, S)
-        for lo, hi in tail_spans:
-            centre(1, lo, hi)
-        for c in range(pieces):
+        centre(0, PIECE, S)
+        centre(1, 0, PIECE)
+        centre(1, PIECE, HALF)
+        weave(0, False)
+        centre(1, HALF, S)
+        quantise(0)
+        for c in range(1, pieces):
             weave(c, c > 1)
-        for c in range(pieces):
+        for c in range(1, pieces):
             quantise(c)
         for c in range(pieces):
             second_product(c)

@@ -22,6 +22,7 @@ P = 128
 PACK = 4
 HALF = S // 2
 PIECE = 128
+THIN = 32
 
 
 def load_scale_rows(queue, plane, rows):
@@ -56,7 +57,24 @@ def tile_picked_deepset_none_p_kernel(tc, x_words, x_scales, w1, w2_words, w2_sc
         x_picked = sb.tile([P, S], U32, name="x_picked", align_bytes=64)
         xs_picked = sb.tile([P, S], U8, name="xs_picked", align_bytes=64)
         nc.vector.tensor_copy(x_picked[:], x_table[:].bitcast(U32).indirect(offsets[:]))
-        nc.vector.tensor_copy(xs_picked[:], xs_table[:].indirect(offsets[:]))
+        for lo, hi in ((0, PIECE), (PIECE, S)):
+            nc.vector.tensor_copy(xs_picked[:, lo:hi], xs_table[:].indirect(offsets[:, lo // 16 : hi // 16]))
+
+        def warm_up(dst, width):
+            nc.tensor.matmul_mx(
+                out=dst,
+                lhsT=x_picked[:, :THIN].bitcast(FP8X4),
+                lhsT_scale=xs_picked[:, :THIN],
+                rhs=x_picked[:, :width].bitcast(FP8X4),
+                rhs_scale=xs_picked[:, :width],
+                start=True,
+                stop=True,
+            )
+
+        warm = [ps.tile([THIN, S], F32, name=f"warm{a}", tag=f"bank{6 + a}") for a in range(2)]
+        for c in range(S // PIECE):
+            warm_up(warm[0][:, c * PIECE : (c + 1) * PIECE], PIECE)
+        warm_up(warm[1][:], S)
 
         w1_src = [tile[:].rearrange("p j (m t) -> p m j t", t=PACK) for tile in w1_raw]
         w1_bf = [sb.tile([P, 2, P, PACK], BF16, name=f"w1_bf{u}", align_bytes=64) for u in range(2)]
@@ -174,16 +192,6 @@ def tile_picked_deepset_none_p_kernel(tc, x_words, x_scales, w1, w2_words, w2_sc
         empty(banks[0][:], scaled[0][:], neg_mean[0][:], True)
         empty(banks[1][:], scaled[1][:], neg_mean[1][:], True)
 
-        warm = ps.tile([64, S], F32, name="warm", tag="bank2")
-        nc.tensor.matmul_mx(
-            out=warm[:],
-            lhsT=w1_codes[last][:, :64].bitcast(FP8X4),
-            lhsT_scale=w1_plane[last][:, :64],
-            rhs=x_picked[:].bitcast(FP8X4),
-            rhs_scale=xs_picked[:],
-            start=True,
-            stop=True,
-        )
         centre(2, 0, S)
         centre(0, 0, PIECE)
         empty(fold[:], folded[:], neg_mean[last][:], False)

@@ -48,9 +48,9 @@ def tile_picked_deepset_none_p_kernel(tc, x_words, x_scales, w1, w2_words, w2_sc
         w1_rows = w1.rearrange("(p j) c -> p j c", j=PACK)
         nc.sync.dma_start(out=x_table[:], in_=x_words[0].rearrange("p n r -> p (n r)").bitcast(I32))
         nc.sync.dma_start(offsets[:], offs)
+        nc.sync.dma_start(out=w1_raw[0][:], in_=w1_rows[:, :, : H // 2])
         load_scale_rows(nc.sync, xs_table, x_scales[0])
-        for u in range(2):
-            nc.sync.dma_start(out=w1_raw[u][:], in_=w1_rows[:, :, u * H // 2 : (u + 1) * H // 2])
+        nc.sync.dma_start(out=w1_raw[1][:], in_=w1_rows[:, :, H // 2 :])
         nc.sync.dma_start(out=w2_codes[:].bitcast(I32), in_=w2_words[0].bitcast(I32))
         load_scale_rows(nc.sync, w2_plane, w2_scales[0])
 

@@ -25,8 +25,8 @@ PIECE = 128
 THIN = 32
 
 
-def load_scale_rows(queue, plane, rows):
-    for r in range(4):
+def load_scale_rows(queues, plane, rows):
+    for r, queue in enumerate(queues):
         queue.dma_start(out=plane[r:P:32, :].bitcast(I32), in_=rows[r:16:4, :].bitcast(I32))
 
 
@@ -39,20 +39,22 @@ def tile_picked_deepset_none_p_kernel(tc, x_words, x_scales, w1, w2_words, w2_sc
         offsets = sb.tile([P, S // 16], U16, name="offsets")
         x_table = sb.tile([P, T], I32, name="x_table", align_bytes=64)
         xs_table = sb.tile([P, T], U8, name="xs_table", align_bytes=64)
-        w1_raw = [sb.tile([P, PACK, H // 2], F32, name=f"w1_raw{u}", align_bytes=64) for u in range(2)]
+        w1_spans = ((0, H // 2), (H // 2, 3 * H // 4), (3 * H // 4, H))
+        w1_raw = [sb.tile([P, PACK, hi - lo], F32, name=f"w1_raw{lo}", align_bytes=64) for lo, hi in w1_spans]
         w2_codes = sb.tile([P, 2 * N], U8, name="w2_codes", align_bytes=64)
         w2_plane = sb.tile([P, N], U8, name="w2_plane", align_bytes=64)
 
         nc.vector.memset(xs_table[:].bitcast(I32), 0)
         nc.vector.memset(w2_plane[:].bitcast(I32), 0)
         w1_rows = w1.rearrange("(p j) c -> p j c", j=PACK)
-        nc.sync.dma_start(out=x_table[:], in_=x_words[0].rearrange("p n r -> p (n r)").bitcast(I32))
         nc.sync.dma_start(offsets[:], offs)
+        nc.sync.dma_start(out=x_table[:], in_=x_words[0].rearrange("p n r -> p (n r)").bitcast(I32))
         nc.sync.dma_start(out=w1_raw[0][:], in_=w1_rows[:, :, : H // 2])
-        load_scale_rows(nc.sync, xs_table, x_scales[0])
-        nc.sync.dma_start(out=w1_raw[1][:], in_=w1_rows[:, :, H // 2 :])
+        load_scale_rows((nc.sync,) * 4, xs_table, x_scales[0])
+        for tile, (lo, hi) in zip(w1_raw[1:], w1_spans[1:]):
+            nc.sync.dma_start(out=tile[:], in_=w1_rows[:, :, lo:hi])
         nc.sync.dma_start(out=w2_codes[:].bitcast(I32), in_=w2_words[0].bitcast(I32))
-        load_scale_rows(nc.sync, w2_plane, w2_scales[0])
+        load_scale_rows((nc.sync,) * 4, w2_plane, w2_scales[0])
 
         x_picked = sb.tile([P, S], U32, name="x_picked", align_bytes=64)
         xs_picked = sb.tile([P, S], U8, name="xs_picked", align_bytes=64)
@@ -77,22 +79,33 @@ def tile_picked_deepset_none_p_kernel(tc, x_words, x_scales, w1, w2_words, w2_sc
         warm_up(warm[1][:], S)
 
         w1_src = [tile[:].rearrange("p j (m t) -> p m j t", t=PACK) for tile in w1_raw]
-        w1_bf = [sb.tile([P, 2, P, PACK], BF16, name=f"w1_bf{u}", align_bytes=64) for u in range(2)]
+        w1_row = [sb.tile([P, 2 * P * PACK], BF16, name=f"w1_row{u}", align_bytes=64) for u in range(2)]
         w1_codes = [sb.tile([P, P], U32, name=f"w1_codes{t}", align_bytes=64) for t in range(PACK)]
         w1_plane = [sb.tile([P, P], U8, name=f"w1_plane{t}", align_bytes=64) for t in range(PACK)]
-        w1_dst = [tile[:].rearrange("p t m j -> p m j t") for tile in w1_bf]
-        low_m = slice(0, P // 2)
-        share = 40
+        w1_dst = [tile[:].rearrange("p (t m j) -> p m j t", t=2, j=PACK) for tile in w1_row]
+        quarter = P // PACK
+
+        def cast(u, lo, hi, on_scalar):
+            load = max(i for i, span in enumerate(w1_spans) if span[0] <= PACK * lo)
+            first = w1_spans[load][0] // PACK
+            src = w1_src[load][:, lo - first : hi - first, :, 2 * u : 2 * u + 2]
+            if on_scalar:
+                nc.scalar.activation(out=w1_dst[u][:, lo:hi], in_=src, func=COPY)
+            else:
+                nc.vector.tensor_copy(out=w1_dst[u][:, lo:hi], in_=src)
+
+        cast(1, 0, 2 * quarter, True)
+        cast(0, 0, quarter, True)
+        cast(1, 2 * quarter, 3 * quarter, True)
+        cast(0, quarter, 2 * quarter, True)
+        cast(0, 2 * quarter, 3 * quarter, True)
         for u in (1, 0):
-            nc.scalar.activation(out=w1_dst[u][:, low_m], in_=w1_src[0][:, :, :, 2 * u : 2 * u + 2], func=COPY)
-        for u in (1, 0):
-            nc.vector.tensor_copy(out=w1_dst[u][:, P // 2 : P // 2 + share], in_=w1_src[1][:, :share, :, 2 * u : 2 * u + 2])
-            nc.scalar.activation(out=w1_dst[u][:, P // 2 + share :], in_=w1_src[1][:, share:, :, 2 * u : 2 * u + 2], func=COPY)
+            cast(u, 3 * quarter, P, False)
         for t in (2, 0, 1, 3):
             nc.vector.quantize_mx(
                 out=w1_codes[t][:].bitcast(FP8X4),
                 scales=w1_plane[t][:],
-                in_=w1_bf[t // 2][:, t % 2].rearrange("p m j -> p (m j)"),
+                in_=w1_row[t // 2][:, PACK * P * (t % 2) : PACK * P * (t % 2 + 1)],
             )
 
         pieces = S // PIECE

@@ -25,8 +25,8 @@ PIECE = 128
 THIN = 32
 
 
-def load_scale_rows(queues, plane, rows):
-    for r, queue in enumerate(queues):
+def load_scale_rows(queue, plane, rows):
+    for r in range(4):
         queue.dma_start(out=plane[r:P:32, :].bitcast(I32), in_=rows[r:16:4, :].bitcast(I32))
 
 
@@ -39,28 +39,29 @@ def tile_picked_deepset_none_p_kernel(tc, x_words, x_scales, w1, w2_words, w2_sc
         offsets = sb.tile([P, S // 16], U16, name="offsets")
         x_table = sb.tile([P, T], I32, name="x_table", align_bytes=64)
         xs_table = sb.tile([P, T], U8, name="xs_table", align_bytes=64)
-        w1_spans = ((0, H // 2), (H // 2, 3 * H // 4), (3 * H // 4, H))
-        w1_raw = [sb.tile([P, PACK, hi - lo], F32, name=f"w1_raw{lo}", align_bytes=64) for lo, hi in w1_spans]
+        w1_raw = [sb.tile([P, PACK, H // 2], F32, name=f"w1_raw{u}", align_bytes=64) for u in range(2)]
         w2_codes = sb.tile([P, 2 * N], U8, name="w2_codes", align_bytes=64)
         w2_plane = sb.tile([P, N], U8, name="w2_plane", align_bytes=64)
 
         nc.vector.memset(xs_table[:].bitcast(I32), 0)
         nc.vector.memset(w2_plane[:].bitcast(I32), 0)
         w1_rows = w1.rearrange("(p j) c -> p j c", j=PACK)
+        x_rows = x_words[0].rearrange("p n r -> p (n r)").bitcast(I32)
+        ahead = 3 * T // 4
         nc.sync.dma_start(offsets[:], offs)
-        nc.sync.dma_start(out=x_table[:], in_=x_words[0].rearrange("p n r -> p (n r)").bitcast(I32))
-        nc.sync.dma_start(out=w1_raw[0][:], in_=w1_rows[:, :, : H // 2])
-        load_scale_rows((nc.sync,) * 4, xs_table, x_scales[0])
-        for tile, (lo, hi) in zip(w1_raw[1:], w1_spans[1:]):
-            nc.sync.dma_start(out=tile[:], in_=w1_rows[:, :, lo:hi])
+        nc.sync.dma_start(out=x_table[:, :ahead], in_=x_rows[:, :ahead])
+        load_scale_rows(nc.sync, xs_table, x_scales[0])
+        nc.sync.dma_start(out=x_table[:, ahead:], in_=x_rows[:, ahead:])
+        for u in range(2):
+            nc.sync.dma_start(out=w1_raw[u][:], in_=w1_rows[:, :, u * H // 2 : (u + 1) * H // 2])
         nc.sync.dma_start(out=w2_codes[:].bitcast(I32), in_=w2_words[0].bitcast(I32))
-        load_scale_rows((nc.sync,) * 4, w2_plane, w2_scales[0])
+        load_scale_rows(nc.sync, w2_plane, w2_scales[0])
 
         x_picked = sb.tile([P, S], U32, name="x_picked", align_bytes=64)
         xs_picked = sb.tile([P, S], U8, name="xs_picked", align_bytes=64)
-        nc.vector.tensor_copy(x_picked[:], x_table[:].bitcast(U32).indirect(offsets[:]))
+        nc.vector.tensor_copy(xs_picked[:], xs_table[:].indirect(offsets[:]))
         for lo, hi in ((0, PIECE), (PIECE, S)):
-            nc.vector.tensor_copy(xs_picked[:, lo:hi], xs_table[:].indirect(offsets[:, lo // 16 : hi // 16]))
+            nc.vector.tensor_copy(x_picked[:, lo:hi], x_table[:].bitcast(U32).indirect(offsets[:, lo // 16 : hi // 16]))
 
         def warm_up(dst, width):
             nc.tensor.matmul_mx(
@@ -79,33 +80,22 @@ def tile_picked_deepset_none_p_kernel(tc, x_words, x_scales, w1, w2_words, w2_sc
         warm_up(warm[1][:], S)
 
         w1_src = [tile[:].rearrange("p j (m t) -> p m j t", t=PACK) for tile in w1_raw]
-        w1_row = [sb.tile([P, 2 * P * PACK], BF16, name=f"w1_row{u}", align_bytes=64) for u in range(2)]
+        w1_bf = [sb.tile([P, 2, P, PACK], BF16, name=f"w1_bf{u}", align_bytes=64) for u in range(2)]
         w1_codes = [sb.tile([P, P], U32, name=f"w1_codes{t}", align_bytes=64) for t in range(PACK)]
         w1_plane = [sb.tile([P, P], U8, name=f"w1_plane{t}", align_bytes=64) for t in range(PACK)]
-        w1_dst = [tile[:].rearrange("p (t m j) -> p m j t", t=2, j=PACK) for tile in w1_row]
-        quarter = P // PACK
-
-        def cast(u, lo, hi, on_scalar):
-            load = max(i for i, span in enumerate(w1_spans) if span[0] <= PACK * lo)
-            first = w1_spans[load][0] // PACK
-            src = w1_src[load][:, lo - first : hi - first, :, 2 * u : 2 * u + 2]
-            if on_scalar:
-                nc.scalar.activation(out=w1_dst[u][:, lo:hi], in_=src, func=COPY)
-            else:
-                nc.vector.tensor_copy(out=w1_dst[u][:, lo:hi], in_=src)
-
-        cast(1, 0, 2 * quarter, True)
-        cast(0, 0, quarter, True)
-        cast(1, 2 * quarter, 3 * quarter, True)
-        cast(0, quarter, 2 * quarter, True)
-        cast(0, 2 * quarter, 3 * quarter, True)
+        w1_dst = [tile[:].rearrange("p t m j -> p m j t") for tile in w1_bf]
+        low_m = slice(0, P // 2)
+        share = 40
         for u in (1, 0):
-            cast(u, 3 * quarter, P, False)
+            nc.scalar.activation(out=w1_dst[u][:, low_m], in_=w1_src[0][:, :, :, 2 * u : 2 * u + 2], func=COPY)
+        for u in (1, 0):
+            nc.vector.tensor_copy(out=w1_dst[u][:, P // 2 : P // 2 + share], in_=w1_src[1][:, :share, :, 2 * u : 2 * u + 2])
+            nc.scalar.activation(out=w1_dst[u][:, P // 2 + share :], in_=w1_src[1][:, share:, :, 2 * u : 2 * u + 2], func=COPY)
         for t in (2, 0, 1, 3):
             nc.vector.quantize_mx(
                 out=w1_codes[t][:].bitcast(FP8X4),
                 scales=w1_plane[t][:],
-                in_=w1_row[t // 2][:, PACK * P * (t % 2) : PACK * P * (t % 2 + 1)],
+                in_=w1_bf[t // 2][:, t % 2].rearrange("p m j -> p (m j)"),
             )
 
         pieces = S // PIECE

@@ -153,6 +153,8 @@ def tile_picked_deepset_none_p_kernel(tc, x_words, x_scales, w1, w2_words, w2_sc
         z_plane = [sb.tile([P, PIECE], U8, name=f"z_plane{c}", align_bytes=64) for c in range(pieces)]
         out_view = out.rearrange("(m p) n -> p m n", p=P)
 
+        back = sb.tile([P, N // P, HALF], F32, name="back", align_bytes=64)
+
         def weave(c, on_scalar):
             src = pair_words[:, c]
             dst = z_bf[c][:].rearrange("p n t -> p (n t)").bitcast(U32).rearrange("p (n u) -> p n u", u=2)
@@ -170,7 +172,7 @@ def tile_picked_deepset_none_p_kernel(tc, x_words, x_scales, w1, w2_words, w2_sc
 
         def second_product(c):
             cols = slice(c * PIECE, (c + 1) * PIECE)
-            result = sb.tile([P, N // P, PIECE], F32, name=f"result{c}", align_bytes=64)
+            result = back[:, :, cols.start - HALF : cols.stop - HALF] if c >= 2 else sb.tile([P, N // P, PIECE], F32, name=f"result{c}", align_bytes=64)
             for m in range(N // P):
                 bank = ps.tile([P, PIECE], F32, name=f"o{c}{m}", tag=f"bank{2 * c + m}")
                 nc.tensor.matmul_mx(
@@ -188,8 +190,10 @@ def tile_picked_deepset_none_p_kernel(tc, x_words, x_scales, w1, w2_words, w2_sc
                     nc.vector.tensor_copy(out=result[:, m, :], in_=bank[:])
                 if c == 0:
                     nc.sync.dma_start(out=out_view[:, m, cols], in_=result[:, m, :])
-            if c > 0:
+            if c == 1:
                 nc.sync.dma_start(out=out_view[:, :, cols], in_=result[:])
+            if c == pieces - 1:
+                nc.sync.dma_start(out=out_view[:, :, HALF:], in_=back[:])
 
         empty(banks[2][:], scaled[2][:], neg_mean[2][:], False)
         empty(banks[0][:], scaled[0][:], neg_mean[0][:], True)

@@ -153,11 +153,11 @@ def tile_picked_deepset_none_p_kernel(tc, x_words, x_scales, w1, w2_words, w2_sc
         z_plane = [sb.tile([P, PIECE], U8, name=f"z_plane{c}", align_bytes=64) for c in range(pieces)]
         out_view = out.rearrange("(m p) n -> p m n", p=P)
 
-        back = sb.tile([P, N // P, HALF], F32, name="back", align_bytes=64)
+        result = [sb.tile([P, N // P, HALF], F32, name=f"result{half}", align_bytes=64) for half in range(2)]
 
-        def weave(c, on_scalar):
-            src = pair_words[:, c]
-            dst = z_bf[c][:].rearrange("p n t -> p (n t)").bitcast(U32).rearrange("p (n u) -> p n u", u=2)
+        def weave(c, on_scalar, members=slice(0, PIECE)):
+            src = pair_words[:, c, members]
+            dst = z_bf[c][:].rearrange("p n t -> p (n t)").bitcast(U32).rearrange("p (n u) -> p n u", u=2)[:, members]
             if on_scalar:
                 nc.scalar.copy(out=dst, in_=src)
             else:
@@ -171,8 +171,7 @@ def tile_picked_deepset_none_p_kernel(tc, x_words, x_scales, w1, w2_words, w2_sc
             )
 
         def second_product(c):
-            cols = slice(c * PIECE, (c + 1) * PIECE)
-            result = back[:, :, cols.start - HALF : cols.stop - HALF] if c >= 2 else sb.tile([P, N // P, PIECE], F32, name=f"result{c}", align_bytes=64)
+            half, lo = divmod(c * PIECE, HALF)
             for m in range(N // P):
                 bank = ps.tile([P, PIECE], F32, name=f"o{c}{m}", tag=f"bank{2 * c + m}")
                 nc.tensor.matmul_mx(
@@ -185,15 +184,11 @@ def tile_picked_deepset_none_p_kernel(tc, x_words, x_scales, w1, w2_words, w2_sc
                     stop=True,
                 )
                 if m == 0 or c == 0:
-                    nc.scalar.copy(out=result[:, m, :], in_=bank[:])
+                    nc.scalar.copy(out=result[half][:, m, lo : lo + PIECE], in_=bank[:])
                 else:
-                    nc.vector.tensor_copy(out=result[:, m, :], in_=bank[:])
-                if c == 0:
-                    nc.sync.dma_start(out=out_view[:, m, cols], in_=result[:, m, :])
-            if c == 1:
-                nc.sync.dma_start(out=out_view[:, :, cols], in_=result[:])
-            if c == pieces - 1:
-                nc.sync.dma_start(out=out_view[:, :, HALF:], in_=back[:])
+                    nc.vector.tensor_copy(out=result[half][:, m, lo : lo + PIECE], in_=bank[:])
+            if lo + PIECE == HALF:
+                nc.sync.dma_start(out=out_view[:, :, half * HALF : (half + 1) * HALF], in_=result[half][:])
 
         empty(banks[2][:], scaled[2][:], neg_mean[2][:], False)
         empty(banks[0][:], scaled[0][:], neg_mean[0][:], True)
@@ -205,14 +200,14 @@ def tile_picked_deepset_none_p_kernel(tc, x_words, x_scales, w1, w2_words, w2_sc
         for lo, hi in tail_spans:
             centre(last, lo, hi, True)
         centre(0, PIECE, S)
-        centre(1, 0, PIECE)
-        centre(1, PIECE, HALF)
-        weave(0, False)
+        centre(1, 0, HALF)
         centre(1, HALF, S)
-        quantise(0)
-        for c in range(1, pieces):
-            weave(c, c > 1)
-        for c in range(1, pieces):
+        weave(0, False)
+        weave(1, False)
+        weave(2, False, slice(0, PIECE // 2))
+        weave(2, True, slice(PIECE // 2, PIECE))
+        weave(3, True)
+        for c in range(pieces):
             quantise(c)
         for c in range(pieces):
             second_product(c)

from contextlib import ExitStack

import concourse.mybir as mybir

K, T, S, H, N = 512, 1024, 512, 512, 256
FLOPS = 2 * K * H * S + 2 * H * N * S

F32 = mybir.dt.float32
BF16 = mybir.dt.bfloat16
I32 = mybir.dt.int32
U32 = mybir.dt.uint32
U16 = mybir.dt.uint16
U8 = mybir.dt.uint8
FP8X4 = mybir.dt.float8_e4m3fn_x4
FP4X4 = mybir.dt.float4_e2m1fn_x4
MULT = mybir.AluOpType.mult
ADD = mybir.AluOpType.add
COPY = mybir.ActivationFunctionType.Copy
IDENT = mybir.ActivationFunctionType.Identity

P = 128
PACK = 4
HALF = S // 2
PIECE = 128
THIN = 32


def load_scale_rows(queue, plane, rows):
    for r in range(4):
        queue.dma_start(out=plane[r:P:32, :].bitcast(I32), in_=rows[r:16:4, :].bitcast(I32))


def tile_picked_deepset_none_p_kernel(tc, x_words, x_scales, w1, w2_words, w2_scales, offs, out):
    nc = tc.nc
    with ExitStack() as ctx:
        sb = ctx.enter_context(tc.tile_pool(name="sb", bufs=1))
        ps = ctx.enter_context(tc.psum_pool(name="ps", bufs=1))

        offsets = sb.tile([P, S // 16], U16, name="offsets")
        x_table = sb.tile([P, T], I32, name="x_table", align_bytes=64)
        xs_table = sb.tile([P, T], U8, name="xs_table", align_bytes=64)
        w1_raw = [sb.tile([P, PACK, H // 2], F32, name=f"w1_raw{u}", align_bytes=64) for u in range(2)]
        w2_codes = sb.tile([P, 2 * N], U8, name="w2_codes", align_bytes=64)
        w2_plane = sb.tile([P, N], U8, name="w2_plane", align_bytes=64)

        nc.vector.memset(xs_table[:].bitcast(I32), 0)
        nc.vector.memset(w2_plane[:].bitcast(I32), 0)
        w1_rows = w1.rearrange("(p j) c -> p j c", j=PACK)
        x_rows = x_words[0].rearrange("p n r -> p (n r)").bitcast(I32)
        ahead = 3 * T // 4
        nc.sync.dma_start(offsets[:], offs)
        nc.sync.dma_start(out=x_table[:, :ahead], in_=x_rows[:, :ahead])
        load_scale_rows(nc.sync, xs_table, x_scales[0])
        nc.sync.dma_start(out=x_table[:, ahead:], in_=x_rows[:, ahead:])
        for u in range(2):
            nc.sync.dma_start(out=w1_raw[u][:], in_=w1_rows[:, :, u * H // 2 : (u + 1) * H // 2])
        nc.sync.dma_start(out=w2_codes[:].bitcast(I32), in_=w2_words[0].bitcast(I32))
        load_scale_rows(nc.sync, w2_plane, w2_scales[0])

        x_picked = sb.tile([P, S], U32, name="x_picked", align_bytes=64)
        xs_picked = sb.tile([P, S], U8, name="xs_picked", align_bytes=64)
        nc.vector.tensor_copy(xs_picked[:], xs_table[:].indirect(offsets[:]))
        for lo, hi in ((0, PIECE), (PIECE, S)):
            nc.vector.tensor_copy(x_picked[:, lo:hi], x_table[:].bitcast(U32).indirect(offsets[:, lo // 16 : hi // 16]))

        def warm_up(dst, width):
            nc.tensor.matmul_mx(
                out=dst,
                lhsT=x_picked[:, :THIN].bitcast(FP8X4),
                lhsT_scale=xs_picked[:, :THIN],
                rhs=x_picked[:, :width].bitcast(FP8X4),
                rhs_scale=xs_picked[:, :width],
                start=True,
                stop=True,
            )

        warm = [ps.tile([THIN, S], F32, name=f"warm{a}", tag=f"bank{6 + a}") for a in range(2)]
        for c in range(S // PIECE):
            warm_up(warm[0][:, c * PIECE : (c + 1) * PIECE], PIECE)
        warm_up(warm[1][:], S)

        w1_src = [tile[:].rearrange("p j (m t) -> p m j t", t=PACK) for tile in w1_raw]
        w1_bf = [sb.tile([P, 2, P, PACK], BF16, name=f"w1_bf{u}", align_bytes=64) for u in range(2)]
        w1_codes = [sb.tile([P, P], U32, name=f"w1_codes{t}", align_bytes=64) for t in range(PACK)]
        w1_plane = [sb.tile([P, P], U8, name=f"w1_plane{t}", align_bytes=64) for t in range(PACK)]
        w1_dst = [tile[:].rearrange("p t m j -> p m j t") for tile in w1_bf]
        low_m = slice(0, P // 2)
        share = 40
        for u in (1, 0):
            nc.scalar.activation(out=w1_dst[u][:, low_m], in_=w1_src[0][:, :, :, 2 * u : 2 * u + 2], func=COPY)
        for u in (1, 0):
            nc.vector.tensor_copy(out=w1_dst[u][:, P // 2 : P // 2 + share], in_=w1_src[1][:, :share, :, 2 * u : 2 * u + 2])
            nc.scalar.activation(out=w1_dst[u][:, P // 2 + share :], in_=w1_src[1][:, share:, :, 2 * u : 2 * u + 2], func=COPY)
        for t in (2, 0, 1, 3):
            nc.vector.quantize_mx(
                out=w1_codes[t][:].bitcast(FP8X4),
                scales=w1_plane[t][:],
                in_=w1_bf[t // 2][:, t % 2].rearrange("p m j -> p (m j)"),
            )

        pieces = S // PIECE
        last = PACK - 1
        scaled = [sb.tile([P, S], F32, name=f"scaled{t}", align_bytes=64) for t in range(last)]
        folded = sb.tile([P, PIECE], F32, name="folded", align_bytes=64)
        neg_mean = [sb.tile([P, 1], F32, name=f"neg_mean{t}") for t in range(PACK)]
        pair_row = sb.tile([P, PACK * S], BF16, name="pair_row", align_bytes=64)
        pairs = pair_row[:].rearrange("p (c u n e) -> p c u n e", u=2, n=PIECE, e=2)
        pair_words = pair_row[:].bitcast(U32).rearrange("p (c u n) -> p c n u", u=2, n=PIECE)

        def first_pass(t, dst, lo, hi, start=True, stop=True):
            nc.tensor.matmul_mx(
                out=dst,
                lhsT=w1_codes[t][:].bitcast(FP8X4),
                lhsT_scale=w1_plane[t][:],
                rhs=x_picked[:, lo:hi].bitcast(FP8X4),
                rhs_scale=xs_picked[:, lo:hi],
                start=start,
                stop=stop,
            )

        banks = [ps.tile([P, S], F32, name=f"h{t}", tag=f"bank{t}") for t in range(last)]
        for t in (2, 0, 1):
            first_pass(t, banks[t][:], 0, S)
        fold = ps.tile([P, PIECE], F32, name="fold", tag="bank3")
        for c in range(pieces):
            first_pass(last, fold[:], c * PIECE, (c + 1) * PIECE, c == 0, c == pieces - 1)
        tail_spans = tuple((c * PIECE, (c + 1) * PIECE) for c in range(pieces))
        tails = [ps.tile([P, hi - lo], F32, name=f"tail{lo}", tag=f"bank{4 + a}") for a, (lo, hi) in enumerate(tail_spans)]
        for a, (lo, hi) in enumerate(tail_spans):
            first_pass(last, tails[a][:], lo, hi)

        def empty(src, dst, total, on_scalar):
            if on_scalar:
                nc.scalar.activation(out=dst, in_=src, func=COPY, scale=-1.0 / S, accum_out=total)
            else:
                nc.vector.tensor_scalar(out=dst, in0=src, scalar1=-1.0 / S, scalar2=None, op0=MULT, op1=ADD, accum_out=total)

        def centre(t, lo, hi, on_scalar=False):
            dst = pairs[:, lo // PIECE : hi // PIECE, t // 2, :, t % 2].rearrange("p c (h n) -> p h c n", h=2)
            if t == last:
                b = max(i for i, span in enumerate(tail_spans) if span[0] <= lo)
                src, factor = tails[b][:, lo - tail_spans[b][0] : hi - tail_spans[b][0]], 1.0
            else:
                src, factor = scaled[t][:, lo:hi], -float(S)
            src = src.rearrange("p (c h n) -> p h c n", h=2, n=PIECE // 2)
            if on_scalar:
                nc.scalar.activation(out=dst, in_=src, func=IDENT, scale=factor, bias=neg_mean[t][:])
            else:
                nc.vector.tensor_scalar(out=dst, in0=src, scalar1=factor, scalar2=neg_mean[t][:], op0=MULT, op1=ADD)

        z_bf = [sb.tile([P, PIECE, PACK], BF16, name=f"z_bf{c}", align_bytes=64) for c in range(pieces)]
        z_codes = [sb.tile([P, PIECE], U32, name=f"z_codes{c}", align_bytes=64) for c in range(pieces)]
        z_plane = [sb.tile([P, PIECE], U8, name=f"z_plane{c}", align_bytes=64) for c in range(pieces)]
        out_view = out.rearrange("(m p) n -> p m n", p=P)

        result = [sb.tile([P, N // P, HALF], F32, name=f"result{half}", align_bytes=64) for half in range(2)]

        def weave(c, on_scalar, members=slice(0, PIECE)):
            src = pair_words[:, c, members]
            dst = z_bf[c][:].rearrange("p n t -> p (n t)").bitcast(U32).rearrange("p (n u) -> p n u", u=2)[:, members]
            if on_scalar:
                nc.scalar.copy(out=dst, in_=src)
            else:
                nc.vector.tensor_copy(out=dst.bitcast(I32), in_=src.bitcast(I32))

        def quantise(c):
            nc.vector.quantize_mx(
                out=z_codes[c][:].bitcast(FP8X4),
                scales=z_plane[c][:],
                in_=z_bf[c][:].rearrange("p n t -> p (n t)"),
            )

        def second_product(c):
            half, lo = divmod(c * PIECE, HALF)
            for m in range(N // P):
                bank = ps.tile([P, PIECE], F32, name=f"o{c}{m}", tag=f"bank{2 * c + m}")
                nc.tensor.matmul_mx(
                    out=bank[:],
                    lhsT=w2_codes[:, 2 * P * m : 2 * P * (m + 1)].bitcast(FP4X4),
                    lhsT_scale=w2_plane[:, P * m : P * (m + 1)],
                    rhs=z_codes[c][:].bitcast(FP8X4),
                    rhs_scale=z_plane[c][:],
                    start=True,
                    stop=True,
                )
                if m == 0 or c == 0:
                    nc.scalar.copy(out=result[half][:, m, lo : lo + PIECE], in_=bank[:])
                else:
                    nc.vector.tensor_copy(out=result[half][:, m, lo : lo + PIECE], in_=bank[:])
            if lo + PIECE == HALF:
                nc.sync.dma_start(out=out_view[:, :, half * HALF : (half + 1) * HALF], in_=result[half][:])

        empty(banks[2][:], scaled[2][:], neg_mean[2][:], False)
        empty(banks[0][:], scaled[0][:], neg_mean[0][:], True)
        empty(banks[1][:], scaled[1][:], neg_mean[1][:], True)

        centre(2, 0, S)
        centre(0, 0, PIECE)
        empty(fold[:], folded[:], neg_mean[last][:], False)
        for lo, hi in tail_spans:
            centre(last, lo, hi, True)
        centre(0, PIECE, S)
        centre(1, 0, HALF)
        centre(1, HALF, S)
        weave(0, False)
        weave(1, False)
        weave(2, False, slice(0, PIECE // 2))
        weave(2, True, slice(PIECE // 2, PIECE))
        weave(3, True)
        for c in range(pieces):
            quantise(c)
        for c in range(pieces):
            second_product(c)
